import numpy as np
import ml_dtypes


def mxq(x, axis, fmt="e4m3"):
    dtype, down = {"e4m3": (ml_dtypes.float8_e4m3fn, 7), "e5m2": (ml_dtypes.float8_e5m2, 14)}[fmt]
    v = np.moveaxis(np.asarray(x, np.float32).astype(ml_dtypes.bfloat16).astype(np.float64), axis, -1)
    blocks = v.reshape(v.shape[:-1] + (-1, 32))
    amax = np.abs(blocks).max(-1, keepdims=True)
    byte = np.maximum(np.where(amax > 0, np.frexp(amax)[1] - 1 + 127, 0) - down, 1)
    scale = np.exp2(byte - 127.0)
    codes = (blocks / scale).astype(np.float32).astype(dtype).astype(np.float64)
    return np.moveaxis((codes * scale).reshape(v.shape), -1, axis)


WIDE = False


def mx_kscale(k):
    if not WIDE:
        return np.ones(k)
    levels = np.array([10, -10, 5, -5, 0])
    if k % 512:
        return np.exp2(np.random.permutation(np.resize(levels, k // 32))).repeat(32)
    a = np.empty((k // 512, 16))
    for p in range(k // 512):
        a[p, :8] = np.random.permutation(np.resize(levels, 8))
        for g in range(8):
            far = levels[np.abs(levels - a[p, g]) >= 10]
            a[p, g + 8] = far[np.random.randint(len(far))]
    return np.exp2(a.ravel()).repeat(32)


def f64(x):
    return np.asarray(x).astype(np.float64)


def striped(idx):
    return np.tile(idx.reshape(-1, 16).T, (8, 1)).astype(np.uint16)


def unstriped(offs):
    return offs[:16].T.reshape(-1).astype(np.int64)


E2M1 = np.array([0.0, 0.5, 1.0, 1.5, 2.0, 3.0, 4.0, 6.0, -0.0, -0.5, -1.0, -1.5, -2.0, -3.0, -4.0, -6.0])


def pack_weight(w, fmt):
    k, n = w.shape
    w = f64(np.asarray(w, np.float32).astype(ml_dtypes.bfloat16)).reshape(k // 32, 32, n)
    amax = np.abs(w).max(1)
    if fmt == "e4m3":
        byte = np.frexp(amax)[1] - 1 + 127 - 7
    else:
        mant, ex = np.frexp(amax / 6.0)
        byte = np.where(mant > 0.5, ex, ex - 1) + 127
    byte = np.clip(np.where(amax > 0, byte, 1), 1, 254)
    scaled = (w * np.exp2(127.0 - byte)[:, None, :]).reshape(k, n).astype(np.float32)
    by_word = np.ascontiguousarray(scaled.reshape(k // 512, 128, 4, n).transpose(0, 1, 3, 2))
    if fmt == "e4m3":
        words = by_word.astype(ml_dtypes.float8_e4m3fn).view(np.uint8)
    else:
        c = by_word.astype(ml_dtypes.float4_e2m1fn).view(np.uint8) & 0xF
        words = (c[..., 0::2] | (c[..., 1::2] << 4)).reshape(k // 512, 128, 2 * n)
    return np.ascontiguousarray(words), np.ascontiguousarray(byte.astype(np.uint8).reshape(k // 512, 16, n))


def unpack_weight(words, scales, fmt):
    g, _, n = scales.shape
    words = np.ascontiguousarray(words).reshape(g, 128, n, -1)
    if fmt == "e4m3":
        vals = words.view(ml_dtypes.float8_e4m3fn).astype(np.float64)
    else:
        nib = np.empty((g, 128, n, 4), np.uint8)
        nib[..., 0::2] = words & 0xF
        nib[..., 1::2] = words >> 4
        vals = E2M1[nib]
    vals = vals * np.repeat(np.exp2(scales.astype(np.float64) - 127.0), 8, axis=1)[..., None]
    return vals.transpose(0, 1, 3, 2).reshape(g * 512, n)


def gelu(v):
    return 0.5 * v * (1.0 + np.tanh(np.sqrt(2.0 / np.pi) * (v + 0.044715 * v**3)))


K, T, S, H, N = 1024, 2048, 1024, 512, 1024

def setup_inputs():
    n = np.random.standard_normal
    s = mx_kscale(K)[:, None]
    u = mx_kscale(H)[:, None]
    tab_words, tab_scales = pack_weight(n((K, T)) * s, "e4m3")
    w1_words, w1_scales = pack_weight(n((K, H)) / np.sqrt(K) / s * u.T, "e2m1")
    return {
        "tab_words": tab_words,
        "tab_scales": tab_scales,
        "w1_words": w1_words,
        "w1_scales": w1_scales,
        "b1": (0.5 * n(H) * u[:, 0]).astype(np.float32),
        "w2": (n((H, N)) / np.sqrt(H) / u).astype(np.float32),
        "lam": np.random.uniform(0.2, 0.9, N).astype(np.float32),
        "gT": n((N, T)).astype(np.float32),
        "offs": striped(np.random.permutation(T)[:S]),
    }

def reference(tab_words, tab_scales, w1_words, w1_scales, b1, w2, lam, gT, offs):
    v = unpack_weight(tab_words, tab_scales, "e4m3")[:, unstriped(offs)]
    w1 = unpack_weight(w1_words, w1_scales, "e2m1")
    h = (w1.T @ v) + f64(b1)[:, None]
    y = mxq(f64(w2), 0, "e4m3").T @ mxq(h, 0, "e4m3")
    g = f64(gT)[:, unstriped(offs)]
    new = g + f64(lam)[:, None] * (y - g)
    out = f64(gT).copy()
    out[:, unstriped(offs)] = new
    return out

@@ -1,0 +1,210 @@
+from contextlib import ExitStack
+
+import concourse.mybir as mybir
+
+K, T, S, H, N = 1024, 2048, 1024, 512, 1024
+FLOPS = 2 * K * H * S + 2 * H * N * S
+
+F32 = mybir.dt.float32
+BF16 = mybir.dt.bfloat16
+I32 = mybir.dt.int32
+U32 = mybir.dt.uint32
+U16 = mybir.dt.uint16
+U8 = mybir.dt.uint8
+E4M3 = mybir.dt.float8_e4m3fn_x4
+E2M1 = mybir.dt.float4_e2m1fn_x4
+COPY = mybir.ActivationFunctionType.Copy
+IDENTITY = mybir.ActivationFunctionType.Identity
+ADD = mybir.AluOpType.add
+
+P = 128
+PACK = 4
+PASSES = K // (P * PACK)
+HALF = 512
+HALVES = S // HALF
+LIST_COLS = HALF // 16
+ROW_TILES = N // P
+EARLY_TILES = 2
+EARLY_COLS = EARLY_TILES * P
+
+
+def tile_list_cine_line_refill_kernel(
+    tc, tab_words, tab_scales, w1_words, w1_scales, b1, w2, lam, gT, offs, out
+):
+    nc = tc.nc
+    with ExitStack() as ctx:
+        keep = ctx.enter_context(tc.tile_pool(name="keep", bufs=1))
+        ring = ctx.enter_context(tc.tile_pool(name="ring", bufs=4))
+        psum_h = ctx.enter_context(tc.psum_pool(name="psum_h", bufs=4))
+        psum_y = ctx.enter_context(tc.psum_pool(name="psum_y", bufs=4))
+
+        offsets = keep.tile([P, S // 16], U16, name="offsets")
+        tab_scale_window = keep.tile([P, T], U8, name="tab_scale_window", align_bytes=64)
+        w1_scales_raw = keep.tile([P, PASSES * H], U8, name="w1_scales_raw", align_bytes=64)
+        v_plane1 = keep.tile([P, S], U8, name="v_plane1", align_bytes=64)
+        nc.vector.memset(tab_scale_window[:].bitcast(I32), 0)
+        nc.vector.memset(w1_scales_raw[:].bitcast(I32), 0)
+        nc.vector.memset(v_plane1[:].bitcast(I32), 0)
+
+        nc.sync.dma_start(offsets[:], offs)
+        w1_raw = keep.tile([P, PASSES, 2 * H], U8, name="w1_raw", align_bytes=64)
+        nc.sync.dma_start(w1_raw[:].bitcast(I32), w1_words.rearrange("a p c -> p a c").bitcast(I32))
+        for q in range(4):
+            nc.sync.dma_start(
+                tab_scale_window[32 * q : 32 * q + 4 * PASSES, :].bitcast(I32),
+                tab_scales[:, 4 * q : 4 * q + 4, :].bitcast(I32),
+            )
+        word_windows = []
+        for a in range(PASSES):
+            window = keep.tile([P, T], U32, name=f"word_window{a}", align_bytes=64)
+            nc.sync.dma_start(window[:].bitcast(I32), tab_words[a].rearrange("p t i -> p (t i)").bitcast(I32))
+            word_windows.append(window)
+        for q in range(4):
+            nc.scalar.dma_start(
+                w1_scales_raw[32 * q : 32 * q + 4, :].rearrange("i (a c) -> i a c", a=PASSES).bitcast(I32),
+                w1_scales[:, 4 * q : 4 * q + 4, :].rearrange("a i c -> i a c").bitcast(I32),
+            )
+        bias = keep.tile([P, PACK], F32, name="bias")
+        nc.scalar.dma_start(bias[:], b1.rearrange("(p t) -> p t", t=PACK))
+
+        w2_rows = w2.rearrange("(p t) n -> p t n", t=PACK)
+        w2_early = keep.tile([P, PACK, EARLY_COLS], F32, name="w2_early")
+        nc.sync.dma_start(w2_early[:], w2_rows[:, :, 0:EARLY_COLS])
+        lines = [keep.tile([P, T], F32, name=f"lines{c}") for c in range(ROW_TILES)]
+        weight = keep.tile([P, ROW_TILES], F32, name="weight")
+        w2_late = keep.tile([P, PACK, N - EARLY_COLS], F32, name="w2_late")
+        for c in range(ROW_TILES):
+            nc.sync.dma_start(lines[c][:], gT[c * P : (c + 1) * P, :])
+            if c == 1:
+                with nc.allow_non_contiguous_dma(reason="one weight for each partition"):
+                    nc.sync.dma_start(weight[:], lam.rearrange("(c p) -> p c", p=P))
+            if c == 3:
+                nc.sync.dma_start(w2_late[:], w2_rows[:, :, EARLY_COLS:N])
+
+        w1_codes = keep.tile([P, PASSES * 2 * H], U8, name="w1_codes", align_bytes=64)
+        nc.vector.tensor_copy(
+            w1_codes[:].bitcast(U16).rearrange("p (a t u i) -> p a u t i", a=PASSES, t=PACK, i=8),
+            w1_raw[:].rearrange("p a c -> p (a c)").bitcast(U16).rearrange("p (a u i t) -> p a u t i", a=PASSES, t=PACK, i=8),
+        )
+        v_plane0 = keep.tile([P, S], U8, name="v_plane0", align_bytes=64)
+        nc.vector.tensor_copy(v_plane0[:], tab_scale_window[:].indirect(offsets[:]))
+        for q in range(4):
+            nc.scalar.dma_start(
+                v_plane1[32 * q : 32 * q + 4, :].bitcast(I32),
+                v_plane0[32 * q + 4 : 32 * q + 8, :].bitcast(I32),
+            )
+        v_planes = [v_plane0, v_plane1]
+        w1_planes = keep.tile([P, PASSES * H], U8, name="w1_planes", align_bytes=64)
+        nc.vector.tensor_copy(
+            w1_planes[:].rearrange("p (a t u i) -> p a u t i", a=PASSES, t=PACK, i=16),
+            w1_scales_raw[:].rearrange("p (a u i t) -> p a u t i", a=PASSES, t=PACK, i=16),
+        )
+
+        def list_half(half):
+            return offsets[:, half * LIST_COLS : (half + 1) * LIST_COLS]
+
+        v_codes = {}
+        for a in range(PASSES):
+            for half in range(HALVES):
+                picked = keep.tile([P, HALF], U32, name=f"v_codes{a}{half}", align_bytes=64)
+                nc.vector.tensor_copy(picked[:], word_windows[a][:].indirect(list_half(half)))
+                v_codes[a, half] = picked
+
+        w2_codes = keep.tile([P, N], U32, name="w2_codes", align_bytes=64)
+        w2_plane = keep.tile([P, N], U8, name="w2_plane", align_bytes=64)
+
+        def quantise_w2(raw, raw_first, first, width):
+            grouped = keep.tile([P, width * PACK], BF16, name=f"w2_grouped{first}", align_bytes=64)
+            nc.scalar.copy(
+                grouped[:].rearrange("p (u i t) -> p u t i", t=PACK, i=4),
+                raw[:, :, raw_first : raw_first + width].rearrange("p t (u i) -> p u t i", i=4),
+            )
+            nc.vector.quantize_mx(
+                out=w2_codes[:, first : first + width].bitcast(E4M3),
+                scales=w2_plane[:, first : first + width],
+                in_=grouped[:],
+            )
+
+        def coefficients(half):
+            cols = slice(half * HALF, (half + 1) * HALF)
+            sums = [psum_h.tile([P, HALF], F32, name="h_sum") for t in range(PACK)]
+            for a in range(PASSES):
+                for t in range(PACK):
+                    first = a * H + t * P
+                    nc.tensor.matmul_mx(
+                        out=sums[t][:],
+                        lhsT=w1_codes[:, 2 * first : 2 * (first + P)].bitcast(E2M1),
+                        lhsT_scale=w1_planes[:, first : first + P],
+                        rhs=v_codes[a, half][:].bitcast(E4M3),
+                        rhs_scale=v_planes[a][:, cols],
+                        start=(a == 0),
+                        stop=(a == PASSES - 1),
+                    )
+            rounded = keep.tile([P, PACK, HALF], BF16, name=f"h_rounded{half}")
+            for t in range(PACK):
+                nc.scalar.activation(rounded[:, t, :], sums[t][:], IDENTITY, bias=bias[:, t : t + 1])
+            grouped = keep.tile([P, HALF * PACK], BF16, name=f"h_grouped{half}", align_bytes=64)
+            nc.scalar.copy(
+                grouped[:].rearrange("p (u i t) -> p u t i", t=PACK, i=4),
+                rounded[:].rearrange("p t (u i) -> p u t i", i=4),
+            )
+            codes = keep.tile([P, HALF], U32, name=f"h_codes{half}", align_bytes=64)
+            plane = keep.tile([P, HALF], U8, name=f"h_plane{half}", align_bytes=64)
+            nc.vector.quantize_mx(out=codes[:].bitcast(E4M3), scales=plane[:], in_=grouped[:])
+            return codes, plane
+
+        held = [keep.tile([P, S], F32, name=f"held{c}") for c in range(ROW_TILES)]
+        rest = keep.tile([P, ROW_TILES], F32, name="rest")
+
+        def gather_lines(c):
+            nc.vector.tensor_copy(held[c][:], lines[c][:].indirect(offsets[:]))
+
+        def weigh_held(c):
+            nc.scalar.activation(held[c][:], held[c][:], COPY, scale=rest[:, c : c + 1])
+
+        def predict(c, h_half, into):
+            codes, plane = h_half
+            cols = slice(c * P, (c + 1) * P)
+            y_sum = psum_y.tile([P, HALF], F32, name="y_sum")
+            nc.tensor.matmul_mx(
+                out=y_sum[:],
+                lhsT=w2_codes[:, cols].bitcast(E4M3),
+                lhsT_scale=w2_plane[:, cols],
+                rhs=codes[:].bitcast(E4M3),
+                rhs_scale=plane[:],
+                start=True,
+                stop=True,
+            )
+            nc.scalar.activation(into, y_sum[:], COPY, scale=weight[:, c : c + 1])
+
+        def store(c):
+            nc.sync.dma_start(out[c * P : (c + 1) * P, :], lines[c][:])
+
+        quantise_w2(w2_early, 0, 0, EARLY_COLS)
+        for c in range(EARLY_TILES + 1):
+            gather_lines(c)
+        nc.scalar.activation(rest[:], weight[:], COPY, scale=-1.0, bias=1.0)
+        h = []
+        for half in range(HALVES):
+            cols = slice(half * HALF, (half + 1) * HALF)
+            h.append(coefficients(half))
+            for c in range(EARLY_TILES):
+                if half == 0:
+                    weigh_held(c)
+                moved = keep.tile([P, HALF], F32, name=f"moved_early{c}{half}")
+                predict(c, h[half], moved[:])
+                nc.vector.tensor_tensor(lines[c][:].indirect(list_half(half)), held[c][:, cols], moved[:], ADD)
+                if half == HALVES - 1:
+                    store(c)
+        quantise_w2(w2_late, 0, EARLY_COLS, 256)
+        for c in range(EARLY_TILES, ROW_TILES):
+            if c + 1 < ROW_TILES:
+                gather_lines(c + 1)
+            if c == 3:
+                quantise_w2(w2_late, 256, 512, 512)
+            weigh_held(c)
+            moved = ring.tile([P, S], F32, name="moved")
+            for half in range(HALVES):
+                predict(c, h[half], moved[:, half * HALF : (half + 1) * HALF])
+            nc.vector.tensor_tensor(lines[c][:].indirect(offsets[:]), held[c][:], moved[:], ADD)
+            store(c)

@@ -1,6 +1,7 @@
 from contextlib import ExitStack
 
 import concourse.mybir as mybir
+from concourse.masks import make_identity
 
 K, T, S, H, N = 1024, 2048, 1024, 512, 1024
 FLOPS = 2 * K * H * S + 2 * H * N * S
@@ -26,6 +27,9 @@ LIST_COLS = HALF // 16
 ROW_TILES = N // P
 EARLY_TILES = 2
 EARLY_COLS = EARLY_TILES * P
+LEAD = 3
+PARKED = 72
+RUN = 8
 
 
 def tile_list_cine_line_refill_kernel(
@@ -34,6 +38,7 @@ def tile_list_cine_line_refill_kernel(
     nc = tc.nc
     with ExitStack() as ctx:
         keep = ctx.enter_context(tc.tile_pool(name="keep", bufs=1))
+        shared = ctx.enter_context(tc.tile_pool(name="shared", bufs=1))
         ring = ctx.enter_context(tc.tile_pool(name="ring", bufs=4))
         psum_h = ctx.enter_context(tc.psum_pool(name="psum_h", bufs=4))
         psum_y = ctx.enter_context(tc.psum_pool(name="psum_y", bufs=4))
@@ -43,62 +48,83 @@ def tile_list_cine_line_refill_kernel(
         w1_scales_raw = keep.tile([P, PASSES * H], U8, name="w1_scales_raw", align_bytes=64)
         v_plane1 = keep.tile([P, S], U8, name="v_plane1", align_bytes=64)
         nc.vector.memset(tab_scale_window[:].bitcast(I32), 0)
-        nc.vector.memset(w1_scales_raw[:].bitcast(I32), 0)
+        nc.gpsimd.memset(w1_scales_raw[:].bitcast(I32), 0)
         nc.vector.memset(v_plane1[:].bitcast(I32), 0)
+        vector_rows = keep.tile([P, P], F32, name="vector_rows")
+        nc.vector.memset(vector_rows[:], 0.0)
 
         nc.sync.dma_start(offsets[:], offs)
         w1_raw = keep.tile([P, PASSES, 2 * H], U8, name="w1_raw", align_bytes=64)
         nc.sync.dma_start(w1_raw[:].bitcast(I32), w1_words.rearrange("a p c -> p a c").bitcast(I32))
         for q in range(4):
             nc.sync.dma_start(
-                tab_scale_window[32 * q : 32 * q + 4 * PASSES, :].bitcast(I32),
-                tab_scales[:, 4 * q : 4 * q + 4, :].bitcast(I32),
+                tab_scale_window[32 * q : 32 * q + 4, :].bitcast(I32),
+                tab_scales[0, 4 * q : 4 * q + 4, :].bitcast(I32),
             )
-        word_windows = []
-        for a in range(PASSES):
-            window = keep.tile([P, T], U32, name=f"word_window{a}", align_bytes=64)
-            nc.sync.dma_start(window[:].bitcast(I32), tab_words[a].rearrange("p t i -> p (t i)").bitcast(I32))
-            word_windows.append(window)
-        for q in range(4):
-            nc.scalar.dma_start(
+        nc.sync.dma_start(tab_scale_window[PARKED : PARKED + 16, :].bitcast(I32), tab_scales[1].bitcast(I32))
+        word_windows = [
+            keep.tile([P, T], U32, name=f"word_window{a}", tag=f"word_window{a}", align_bytes=64) for a in range(PASSES)
+        ]
+        lines = [keep.tile([P, T], F32, name=f"lines{c}") for c in range(ROW_TILES)]
+
+        def load_words(a):
+            nc.sync.dma_start(
+                word_windows[a][:].bitcast(I32), tab_words[a].rearrange("p t i -> p (t i)").bitcast(I32)
+            )
+
+        def load_w1_scales(q):
+            nc.sync.dma_start(
                 w1_scales_raw[32 * q : 32 * q + 4, :].rearrange("i (a c) -> i a c", a=PASSES).bitcast(I32),
                 w1_scales[:, 4 * q : 4 * q + 4, :].rearrange("a i c -> i a c").bitcast(I32),
             )
-        bias = keep.tile([P, PACK], F32, name="bias")
-        nc.scalar.dma_start(bias[:], b1.rearrange("(p t) -> p t", t=PACK))
 
-        w2_rows = w2.rearrange("(p t) n -> p t n", t=PACK)
-        w2_early = keep.tile([P, PACK, EARLY_COLS], F32, name="w2_early")
-        nc.sync.dma_start(w2_early[:], w2_rows[:, :, 0:EARLY_COLS])
-        lines = [keep.tile([P, T], F32, name=f"lines{c}") for c in range(ROW_TILES)]
-        weight = keep.tile([P, ROW_TILES], F32, name="weight")
-        w2_late = keep.tile([P, PACK, N - EARLY_COLS], F32, name="w2_late")
-        for c in range(ROW_TILES):
+        def load_lines(c):
             nc.sync.dma_start(lines[c][:], gT[c * P : (c + 1) * P, :])
+
+        load_words(0)
+        for q in range(4):
+            load_w1_scales(q)
+        load_words(1)
+        load_lines(0)
+        nc.sync.dma_start(
+            vector_rows[0:PACK, :].rearrange("t (b j) -> t b j", j=RUN),
+            b1.rearrange("(b t j) -> t b j", t=PACK, j=RUN),
+        )
+        nc.sync.dma_start(vector_rows[PACK : PACK + ROW_TILES, :], lam.rearrange("(c p) -> c p", p=P))
+        identity = keep.tile([P, P], F32, name="identity")
+        make_identity(nc, identity[:])
+        turned = psum_y.tile([P, HALF], F32, name="y_sum")
+        nc.tensor.transpose(turned[:, 0:P], vector_rows[:], identity[:])
+        columns = keep.tile([P, PACK + ROW_TILES], F32, name="columns")
+        nc.scalar.copy(columns[:], turned[:, 0 : PACK + ROW_TILES])
+        bias = columns[:, 0:PACK]
+        weight = columns[:, PACK : PACK + ROW_TILES]
+
+        w2_rows = w2.rearrange("(b t j) n -> t b j n", t=PACK, j=RUN)
+        w2_early = keep.tile([P, PACK, EARLY_COLS], F32, name="w2_early")
+        w2_late = keep.tile([P, PACK, N - EARLY_COLS], F32, name="w2_late")
+        for c in range(1, ROW_TILES):
+            load_lines(c)
             if c == 1:
-                with nc.allow_non_contiguous_dma(reason="one weight for each partition"):
-                    nc.sync.dma_start(weight[:], lam.rearrange("(c p) -> p c", p=P))
+                for t in range(PACK):
+                    nc.sync.dma_start(w2_early[:, t, :], w2_rows[t, :, :, 0:EARLY_COLS])
             if c == 3:
-                nc.sync.dma_start(w2_late[:], w2_rows[:, :, EARLY_COLS:N])
+                for t in range(PACK):
+                    nc.sync.dma_start(w2_late[:, t, :], w2_rows[t, :, :, EARLY_COLS:N])
 
         w1_codes = keep.tile([P, PASSES * 2 * H], U8, name="w1_codes", align_bytes=64)
         nc.vector.tensor_copy(
-            w1_codes[:].bitcast(U16).rearrange("p (a t u i) -> p a u t i", a=PASSES, t=PACK, i=8),
-            w1_raw[:].rearrange("p a c -> p (a c)").bitcast(U16).rearrange("p (a u i t) -> p a u t i", a=PASSES, t=PACK, i=8),
+            w1_codes[:].bitcast(I32).rearrange("p (a t b w) -> p a t b w", a=PASSES, t=PACK, w=4),
+            w1_raw[:].bitcast(I32).rearrange("p a (b t w) -> p a t b w", t=PACK, w=4),
         )
         v_plane0 = keep.tile([P, S], U8, name="v_plane0", align_bytes=64)
         nc.vector.tensor_copy(v_plane0[:], tab_scale_window[:].indirect(offsets[:]))
         for q in range(4):
             nc.scalar.dma_start(
                 v_plane1[32 * q : 32 * q + 4, :].bitcast(I32),
-                v_plane0[32 * q + 4 : 32 * q + 8, :].bitcast(I32),
+                v_plane0[PARKED + 4 * q : PARKED + 4 * q + 4, :].bitcast(I32),
             )
         v_planes = [v_plane0, v_plane1]
-        w1_planes = keep.tile([P, PASSES * H], U8, name="w1_planes", align_bytes=64)
-        nc.vector.tensor_copy(
-            w1_planes[:].rearrange("p (a t u i) -> p a u t i", a=PASSES, t=PACK, i=16),
-            w1_scales_raw[:].rearrange("p (a u i t) -> p a u t i", a=PASSES, t=PACK, i=16),
-        )
 
         def list_half(half):
             return offsets[:, half * LIST_COLS : (half + 1) * LIST_COLS]
@@ -109,20 +135,26 @@ def tile_list_cine_line_refill_kernel(
                 picked = keep.tile([P, HALF], U32, name=f"v_codes{a}{half}", align_bytes=64)
                 nc.vector.tensor_copy(picked[:], word_windows[a][:].indirect(list_half(half)))
                 v_codes[a, half] = picked
+            if a == 0:
+                w1_planes = keep.tile([P, PASSES * H], U8, name="w1_planes", tag="word_window0", align_bytes=64)
+                nc.vector.tensor_copy(
+                    w1_planes[:].bitcast(I32).rearrange("p (a t b w) -> p a t b w", a=PASSES, t=PACK, w=2),
+                    w1_scales_raw[:].bitcast(I32).rearrange("p (a b t w) -> p a t b w", a=PASSES, t=PACK, w=2),
+                )
 
         w2_codes = keep.tile([P, N], U32, name="w2_codes", align_bytes=64)
         w2_plane = keep.tile([P, N], U8, name="w2_plane", align_bytes=64)
 
-        def quantise_w2(raw, raw_first, first, width):
-            grouped = keep.tile([P, width * PACK], BF16, name=f"w2_grouped{first}", align_bytes=64)
+        def quantise_w2(raw, rounded, raw_first, first, width):
+            grouped = rounded[:, raw_first * PACK : (raw_first + width) * PACK]
             nc.scalar.copy(
-                grouped[:].rearrange("p (u i t) -> p u t i", t=PACK, i=4),
+                grouped.rearrange("p (u i t) -> p u t i", t=PACK, i=4),
                 raw[:, :, raw_first : raw_first + width].rearrange("p t (u i) -> p u t i", i=4),
             )
             nc.vector.quantize_mx(
                 out=w2_codes[:, first : first + width].bitcast(E4M3),
                 scales=w2_plane[:, first : first + width],
-                in_=grouped[:],
+                in_=grouped,
             )
 
         def coefficients(half):
@@ -140,10 +172,10 @@ def tile_list_cine_line_refill_kernel(
                         start=(a == 0),
                         stop=(a == PASSES - 1),
                     )
-            rounded = keep.tile([P, PACK, HALF], BF16, name=f"h_rounded{half}")
+            rounded = shared.tile([P, PACK, HALF], BF16, name=f"h_rounded{half}", offset=(2048, 4160)[half], align_bytes=64)
             for t in range(PACK):
                 nc.scalar.activation(rounded[:, t, :], sums[t][:], IDENTITY, bias=bias[:, t : t + 1])
-            grouped = keep.tile([P, HALF * PACK], BF16, name=f"h_grouped{half}", align_bytes=64)
+            grouped = keep.tile([P, HALF * PACK], BF16, name=f"h_grouped{half}", tag=f"h_grouped{half}", align_bytes=64)
             nc.scalar.copy(
                 grouped[:].rearrange("p (u i t) -> p u t i", t=PACK, i=4),
                 rounded[:].rearrange("p t (u i) -> p u t i", i=4),
@@ -153,10 +185,14 @@ def tile_list_cine_line_refill_kernel(
             nc.vector.quantize_mx(out=codes[:].bitcast(E4M3), scales=plane[:], in_=grouped[:])
             return codes, plane
 
-        held = [keep.tile([P, S], F32, name=f"held{c}") for c in range(ROW_TILES)]
-        rest = keep.tile([P, ROW_TILES], F32, name="rest")
+        held = {}
+        follows = {4: "h_grouped1", 5: "held1", 6: "held2", 7: "held0"}
 
         def gather_lines(c):
+            if c in (3, 7):
+                held[c] = shared.tile([P, S], F32, name=f"held{c}", offset=0, align_bytes=64)
+            else:
+                held[c] = keep.tile([P, S], F32, name=f"held{c}", tag=follows.get(c, f"held{c}"), align_bytes=64)
             nc.vector.tensor_copy(held[c][:], lines[c][:].indirect(offsets[:]))
 
         def weigh_held(c):
@@ -180,14 +216,19 @@ def tile_list_cine_line_refill_kernel(
         def store(c):
             nc.sync.dma_start(out[c * P : (c + 1) * P, :], lines[c][:])
 
-        quantise_w2(w2_early, 0, 0, EARLY_COLS)
-        for c in range(EARLY_TILES + 1):
+        for c in range(LEAD):
             gather_lines(c)
-        nc.scalar.activation(rest[:], weight[:], COPY, scale=-1.0, bias=1.0)
         h = []
         for half in range(HALVES):
             cols = slice(half * HALF, (half + 1) * HALF)
             h.append(coefficients(half))
+            if half == 0:
+                w2_early_rounded = shared.tile([P, EARLY_COLS * PACK], BF16, name="w2_early_rounded", offset=2048, align_bytes=64)
+                quantise_w2(w2_early, w2_early_rounded, 0, 0, EARLY_COLS)
+            gather_lines(LEAD + half)
+            if half == 0:
+                rest = shared.tile([P, ROW_TILES], F32, name="rest", offset=4096, align_bytes=64)
+                nc.scalar.activation(rest[:], weight, COPY, scale=-1.0, bias=1.0)
             for c in range(EARLY_TILES):
                 if half == 0:
                     weigh_held(c)
@@ -196,12 +237,12 @@ def tile_list_cine_line_refill_kernel(
                 nc.vector.tensor_tensor(lines[c][:].indirect(list_half(half)), held[c][:, cols], moved[:], ADD)
                 if half == HALVES - 1:
                     store(c)
-        quantise_w2(w2_late, 0, EARLY_COLS, 256)
+        w2_late_rounded = shared.tile([P, (N - EARLY_COLS) * PACK], BF16, name="w2_late_rounded", offset=4160, align_bytes=64)
+        quantise_w2(w2_late, w2_late_rounded, 0, EARLY_COLS, 256)
+        quantise_w2(w2_late, w2_late_rounded, 256, 512, 512)
         for c in range(EARLY_TILES, ROW_TILES):
-            if c + 1 < ROW_TILES:
-                gather_lines(c + 1)
-            if c == 3:
-                quantise_w2(w2_late, 256, 512, 512)
+            if c + LEAD < ROW_TILES:
+                gather_lines(c + LEAD)
             weigh_held(c)
             moved = ring.tile([P, S], F32, name="moved")
             for half in range(HALVES):

@@ -20,16 +20,40 @@ ADD = mybir.AluOpType.add
 
 P = 128
 PACK = 4
+QUADRANTS = 4
+RUN = 8
 PASSES = K // (P * PACK)
 HALF = 512
 HALVES = S // HALF
 LIST_COLS = HALF // 16
 ROW_TILES = N // P
+ALIGN = 64
+PARKED = 72
 EARLY_TILES = 2
 EARLY_COLS = EARLY_TILES * P
 LEAD = 3
-PARKED = 72
-RUN = 8
+LATE_WIDTHS = (256, 512)
+MOVED_BUFS = 4
+BANKS = 4
+
+LINE_BYTES = 4 * T
+LINES1_AT = 0
+SCALE_WINDOW_AT = LINES1_AT + LINE_BYTES - ALIGN
+LINES2_AT = SCALE_WINDOW_AT + T - ALIGN
+LINES3_AT = LINES2_AT + LINE_BYTES
+WINDOW0_AT = LINES3_AT + LINE_BYTES - ALIGN
+LINES4_AT = WINDOW0_AT + 4 * T - ALIGN
+LINES5_AT = LINES4_AT + LINE_BYTES
+WINDOW1_AT = LINES5_AT + LINE_BYTES - ALIGN
+LINES6_AT = WINDOW1_AT + 4 * T - ALIGN
+LINES7_AT = LINES6_AT + LINE_BYTES
+LAST_CODES_AT = LINES7_AT + LINE_BYTES - ALIGN
+W2_LATE_AT = LAST_CODES_AT + 4 * HALF - ALIGN
+LINES_AT = (None, LINES1_AT, LINES2_AT, LINES3_AT, LINES4_AT, LINES5_AT, LINES6_AT, LINES7_AT)
+W1_PLANES_AT = WINDOW0_AT + ALIGN
+W2_EARLY_AT = W1_PLANES_AT + PASSES * H
+LAM_ROWS_AT = W2_EARLY_AT + 4 * PACK * EARLY_COLS
+H_ROUNDED1_AT = LAM_ROWS_AT + 4 * P - 2 * PACK * HALF
 
 
 def tile_list_cine_line_refill_kernel(
@@ -38,128 +62,142 @@ def tile_list_cine_line_refill_kernel(
     nc = tc.nc
     with ExitStack() as ctx:
         keep = ctx.enter_context(tc.tile_pool(name="keep", bufs=1))
-        shared = ctx.enter_context(tc.tile_pool(name="shared", bufs=1))
-        ring = ctx.enter_context(tc.tile_pool(name="ring", bufs=4))
-        psum_h = ctx.enter_context(tc.psum_pool(name="psum_h", bufs=4))
-        psum_y = ctx.enter_context(tc.psum_pool(name="psum_y", bufs=4))
+        staged = ctx.enter_context(tc.tile_pool(name="staged", bufs=1))
+        ring = ctx.enter_context(tc.tile_pool(name="ring", bufs=MOVED_BUFS))
+        psum_h = ctx.enter_context(tc.psum_pool(name="psum_h", bufs=BANKS))
+        psum_y = ctx.enter_context(tc.psum_pool(name="psum_y", bufs=BANKS))
+
+        def placed(shape, dtype, name, at):
+            return staged.tile(shape, dtype, name=name, offset=at, align_bytes=ALIGN)
+
+        def kept(shape, dtype, name, after=None):
+            return keep.tile(shape, dtype, name=name, tag=after or name, align_bytes=ALIGN)
 
         offsets = keep.tile([P, S // 16], U16, name="offsets")
-        tab_scale_window = keep.tile([P, T], U8, name="tab_scale_window", align_bytes=64)
-        w1_scales_raw = keep.tile([P, PASSES * H], U8, name="w1_scales_raw", align_bytes=64)
-        v_plane1 = keep.tile([P, S], U8, name="v_plane1", align_bytes=64)
-        nc.vector.memset(tab_scale_window[:].bitcast(I32), 0)
+        scale_window = placed([P, T], U8, "scale_window", SCALE_WINDOW_AT)
+        w1_scales_raw = kept([P, PASSES * H], U8, "w1_scales_raw")
+        v_plane1 = kept([P, S], U8, "v_plane1")
+        bias_rows = kept([P, P], F32, "bias_rows")
+        nc.vector.memset(scale_window[:].bitcast(I32), 0)
         nc.gpsimd.memset(w1_scales_raw[:].bitcast(I32), 0)
         nc.vector.memset(v_plane1[:].bitcast(I32), 0)
-        vector_rows = keep.tile([P, P], F32, name="vector_rows")
-        nc.vector.memset(vector_rows[:], 0.0)
+        nc.vector.memset(bias_rows[:], 0.0)
 
         nc.sync.dma_start(offsets[:], offs)
-        w1_raw = keep.tile([P, PASSES, 2 * H], U8, name="w1_raw", align_bytes=64)
+        w1_raw = kept([P, PASSES, 2 * H], U8, "w1_raw")
         nc.sync.dma_start(w1_raw[:].bitcast(I32), w1_words.rearrange("a p c -> p a c").bitcast(I32))
-        for q in range(4):
+        for q in range(QUADRANTS):
             nc.sync.dma_start(
-                tab_scale_window[32 * q : 32 * q + 4, :].bitcast(I32),
-                tab_scales[0, 4 * q : 4 * q + 4, :].bitcast(I32),
+                scale_window[32 * q : 32 * q + PACK, :].bitcast(I32),
+                tab_scales[0, PACK * q : PACK * (q + 1), :].bitcast(I32),
             )
-        nc.sync.dma_start(tab_scale_window[PARKED : PARKED + 16, :].bitcast(I32), tab_scales[1].bitcast(I32))
-        word_windows = [
-            keep.tile([P, T], U32, name=f"word_window{a}", tag=f"word_window{a}", align_bytes=64) for a in range(PASSES)
-        ]
-        lines = [keep.tile([P, T], F32, name=f"lines{c}") for c in range(ROW_TILES)]
+        nc.sync.dma_start(scale_window[PARKED : PARKED + PACK * QUADRANTS, :].bitcast(I32), tab_scales[1].bitcast(I32))
+        word_windows = [placed([P, T], U32, f"word_window{a}", (WINDOW0_AT, WINDOW1_AT)[a]) for a in range(PASSES)]
+        lines = {}
 
         def load_words(a):
-            nc.sync.dma_start(
-                word_windows[a][:].bitcast(I32), tab_words[a].rearrange("p t i -> p (t i)").bitcast(I32)
-            )
-
-        def load_w1_scales(q):
-            nc.sync.dma_start(
-                w1_scales_raw[32 * q : 32 * q + 4, :].rearrange("i (a c) -> i a c", a=PASSES).bitcast(I32),
-                w1_scales[:, 4 * q : 4 * q + 4, :].rearrange("a i c -> i a c").bitcast(I32),
-            )
+            nc.sync.dma_start(word_windows[a][:].bitcast(I32), tab_words[a].rearrange("p t i -> p (t i)").bitcast(I32))
 
         def load_lines(c):
+            name = f"lines{c}"
+            lines[c] = kept([P, T], F32, name) if LINES_AT[c] is None else placed([P, T], F32, name, LINES_AT[c])
             nc.sync.dma_start(lines[c][:], gT[c * P : (c + 1) * P, :])
 
         load_words(0)
-        for q in range(4):
-            load_w1_scales(q)
+        for q in range(QUADRANTS):
+            nc.sync.dma_start(
+                w1_scales_raw[32 * q : 32 * q + PACK, :].rearrange("i (a c) -> i a c", a=PASSES).bitcast(I32),
+                w1_scales[:, PACK * q : PACK * (q + 1), :].rearrange("a i c -> i a c").bitcast(I32),
+            )
         load_words(1)
         load_lines(0)
         nc.sync.dma_start(
-            vector_rows[0:PACK, :].rearrange("t (b j) -> t b j", j=RUN),
+            bias_rows[0:PACK, :].rearrange("t (b j) -> t b j", j=RUN),
             b1.rearrange("(b t j) -> t b j", t=PACK, j=RUN),
         )
-        nc.sync.dma_start(vector_rows[PACK : PACK + ROW_TILES, :], lam.rearrange("(c p) -> c p", p=P))
-        identity = keep.tile([P, P], F32, name="identity")
+
+        identity = kept([P, P], F32, "identity")
         make_identity(nc, identity[:])
-        turned = psum_y.tile([P, HALF], F32, name="y_sum")
-        nc.tensor.transpose(turned[:, 0:P], vector_rows[:], identity[:])
-        columns = keep.tile([P, PACK + ROW_TILES], F32, name="columns")
-        nc.scalar.copy(columns[:], turned[:, 0 : PACK + ROW_TILES])
-        bias = columns[:, 0:PACK]
-        weight = columns[:, PACK : PACK + ROW_TILES]
 
-        w2_rows = w2.rearrange("(b t j) n -> t b j n", t=PACK, j=RUN)
-        w2_early = keep.tile([P, PACK, EARLY_COLS], F32, name="w2_early")
-        w2_late = keep.tile([P, PACK, N - EARLY_COLS], F32, name="w2_late")
-        for c in range(1, ROW_TILES):
-            load_lines(c)
-            if c == 1:
-                for t in range(PACK):
-                    nc.sync.dma_start(w2_early[:, t, :], w2_rows[t, :, :, 0:EARLY_COLS])
-            if c == 3:
-                for t in range(PACK):
-                    nc.sync.dma_start(w2_late[:, t, :], w2_rows[t, :, :, EARLY_COLS:N])
+        def turn(rows):
+            turned = psum_y.tile([P, HALF], F32, name="y_bank")
+            nc.tensor.transpose(turned[:, 0:P], rows[:], identity[:])
+            return turned
 
-        w1_codes = keep.tile([P, PASSES * 2 * H], U8, name="w1_codes", align_bytes=64)
-        nc.vector.tensor_copy(
-            w1_codes[:].bitcast(I32).rearrange("p (a t b w) -> p a t b w", a=PASSES, t=PACK, w=4),
-            w1_raw[:].bitcast(I32).rearrange("p a (b t w) -> p a t b w", t=PACK, w=4),
-        )
-        v_plane0 = keep.tile([P, S], U8, name="v_plane0", align_bytes=64)
-        nc.vector.tensor_copy(v_plane0[:], tab_scale_window[:].indirect(offsets[:]))
-        for q in range(4):
-            nc.scalar.dma_start(
-                v_plane1[32 * q : 32 * q + 4, :].bitcast(I32),
-                v_plane0[PARKED + 4 * q : PARKED + 4 * q + 4, :].bitcast(I32),
+        bias = kept([P, PACK], F32, "bias")
+        nc.scalar.copy(bias[:], turn(bias_rows)[:, 0:PACK])
+
+        def reorder_columns(into, raw, words):
+            nc.vector.tensor_copy(
+                into.bitcast(I32).rearrange("p (a t b w) -> p a t b w", a=PASSES, t=PACK, w=words),
+                raw.bitcast(I32).rearrange("p (a b t w) -> p a t b w", a=PASSES, t=PACK, w=words),
+            )
+
+        w1_codes = kept([P, PASSES * 2 * H], U8, "w1_codes")
+        reorder_columns(w1_codes[:], w1_raw[:].rearrange("p a c -> p (a c)"), 2 * RUN // 4)
+
+        v_plane0 = kept([P, S], U8, "v_plane0")
+        nc.vector.tensor_copy(v_plane0[:], scale_window[:].indirect(offsets[:]))
+        for q in range(QUADRANTS):
+            nc.sync.dma_start(
+                v_plane1[32 * q : 32 * q + PACK, :].bitcast(I32),
+                v_plane0[PARKED + PACK * q : PARKED + PACK * (q + 1), :].bitcast(I32),
             )
         v_planes = [v_plane0, v_plane1]
 
         def list_half(half):
             return offsets[:, half * LIST_COLS : (half + 1) * LIST_COLS]
 
-        v_codes = {}
-        for a in range(PASSES):
-            for half in range(HALVES):
-                picked = keep.tile([P, HALF], U32, name=f"v_codes{a}{half}", align_bytes=64)
-                nc.vector.tensor_copy(picked[:], word_windows[a][:].indirect(list_half(half)))
-                v_codes[a, half] = picked
-            if a == 0:
-                w1_planes = keep.tile([P, PASSES * H], U8, name="w1_planes", tag="word_window0", align_bytes=64)
-                nc.vector.tensor_copy(
-                    w1_planes[:].bitcast(I32).rearrange("p (a t b w) -> p a t b w", a=PASSES, t=PACK, w=2),
-                    w1_scales_raw[:].bitcast(I32).rearrange("p (a b t w) -> p a t b w", a=PASSES, t=PACK, w=2),
-                )
+        def entries(half):
+            return slice(half * HALF, (half + 1) * HALF)
 
-        w2_codes = keep.tile([P, N], U32, name="w2_codes", align_bytes=64)
-        w2_plane = keep.tile([P, N], U8, name="w2_plane", align_bytes=64)
+        v_codes0 = kept([P, S], U32, "v_codes0")
+        nc.vector.tensor_copy(v_codes0[:], word_windows[0][:].indirect(offsets[:]))
+        w1_planes = placed([P, PASSES * H], U8, "w1_planes", W1_PLANES_AT)
+        reorder_columns(w1_planes[:], w1_scales_raw[:], RUN // 4)
+        v_codes1 = [kept([P, HALF], U32, "v_codes1_first"), placed([P, HALF], U32, "v_codes1_last", LAST_CODES_AT)]
+        for half in range(HALVES):
+            nc.vector.tensor_copy(v_codes1[half][:], word_windows[1][:].indirect(list_half(half)))
 
-        def quantise_w2(raw, rounded, raw_first, first, width):
-            grouped = rounded[:, raw_first * PACK : (raw_first + width) * PACK]
+        w2_rows = w2.rearrange("(b t j) n -> t b j n", t=PACK, j=RUN)
+
+        def load_w2(name, at, first, width):
+            raw = placed([P, PACK, width], F32, name, at)
+            for t in range(PACK):
+                nc.sync.dma_start(raw[:, t, :], w2_rows[t, :, :, first : first + width])
+            return raw
+
+        for c in range(1, LEAD):
+            load_lines(c)
+        w2_early = load_w2("w2_early", W2_EARLY_AT, 0, EARLY_COLS)
+        load_lines(LEAD)
+        lam_rows = placed([P, P], F32, "lam_rows", LAM_ROWS_AT)
+        nc.gpsimd.memset(lam_rows[:], 0.0)
+        nc.sync.dma_start(lam_rows[0:ROW_TILES, :], lam.rearrange("(c p) -> c p", p=P))
+        for c in range(LEAD + 1, ROW_TILES - 1):
+            load_lines(c)
+
+        def interleave(grouped, slots):
             nc.scalar.copy(
-                grouped.rearrange("p (u i t) -> p u t i", t=PACK, i=4),
-                raw[:, :, raw_first : raw_first + width].rearrange("p t (u i) -> p u t i", i=4),
+                grouped[:].rearrange("p (u i t) -> p u t i", t=PACK, i=4),
+                slots.rearrange("p t (u i) -> p u t i", i=4),
             )
+
+        w2_codes = kept([P, N], U32, "w2_codes")
+        w2_plane = kept([P, N], U8, "w2_plane")
+
+        def quantise_w2(slots, first, width, name, after):
+            grouped = kept([P, width * PACK], BF16, name, after)
+            interleave(grouped, slots)
             nc.vector.quantize_mx(
                 out=w2_codes[:, first : first + width].bitcast(E4M3),
                 scales=w2_plane[:, first : first + width],
-                in_=grouped,
+                in_=grouped[:],
             )
 
-        def coefficients(half):
-            cols = slice(half * HALF, (half + 1) * HALF)
-            sums = [psum_h.tile([P, HALF], F32, name="h_sum") for t in range(PACK)]
+        def make_h(half, rounded):
+            sums = [psum_h.tile([P, HALF], F32, name="h_bank") for t in range(PACK)]
+            moving = [v_codes0[:, entries(half)], v_codes1[half][:]]
             for a in range(PASSES):
                 for t in range(PACK):
                     first = a * H + t * P
@@ -167,45 +205,40 @@ def tile_list_cine_line_refill_kernel(
                         out=sums[t][:],
                         lhsT=w1_codes[:, 2 * first : 2 * (first + P)].bitcast(E2M1),
                         lhsT_scale=w1_planes[:, first : first + P],
-                        rhs=v_codes[a, half][:].bitcast(E4M3),
-                        rhs_scale=v_planes[a][:, cols],
+                        rhs=moving[a].bitcast(E4M3),
+                        rhs_scale=v_planes[a][:, entries(half)],
                         start=(a == 0),
                         stop=(a == PASSES - 1),
                     )
-            rounded = shared.tile([P, PACK, HALF], BF16, name=f"h_rounded{half}", offset=(2048, 4160)[half], align_bytes=64)
             for t in range(PACK):
                 nc.scalar.activation(rounded[:, t, :], sums[t][:], IDENTITY, bias=bias[:, t : t + 1])
-            grouped = keep.tile([P, HALF * PACK], BF16, name=f"h_grouped{half}", tag=f"h_grouped{half}", align_bytes=64)
-            nc.scalar.copy(
-                grouped[:].rearrange("p (u i t) -> p u t i", t=PACK, i=4),
-                rounded[:].rearrange("p t (u i) -> p u t i", i=4),
-            )
-            codes = keep.tile([P, HALF], U32, name=f"h_codes{half}", align_bytes=64)
-            plane = keep.tile([P, HALF], U8, name=f"h_plane{half}", align_bytes=64)
+            grouped = kept([P, HALF * PACK], BF16, f"h_grouped{half}")
+            interleave(grouped, rounded[:])
+            return grouped
+
+        def quantise_h(half, grouped, after=None):
+            codes = kept([P, HALF], U32, f"h_codes{half}", after)
+            plane = kept([P, HALF], U8, f"h_plane{half}")
             nc.vector.quantize_mx(out=codes[:].bitcast(E4M3), scales=plane[:], in_=grouped[:])
             return codes, plane
 
         held = {}
-        follows = {4: "h_grouped1", 5: "held1", 6: "held2", 7: "held0"}
 
-        def gather_lines(c):
-            if c in (3, 7):
-                held[c] = shared.tile([P, S], F32, name=f"held{c}", offset=0, align_bytes=64)
-            else:
-                held[c] = keep.tile([P, S], F32, name=f"held{c}", tag=follows.get(c, f"held{c}"), align_bytes=64)
+        def gather_lines(c, after=None):
+            held[c] = kept([P, S], F32, f"held{c}", after)
             nc.vector.tensor_copy(held[c][:], lines[c][:].indirect(offsets[:]))
 
         def weigh_held(c):
             nc.scalar.activation(held[c][:], held[c][:], COPY, scale=rest[:, c : c + 1])
 
-        def predict(c, h_half, into):
-            codes, plane = h_half
-            cols = slice(c * P, (c + 1) * P)
-            y_sum = psum_y.tile([P, HALF], F32, name="y_sum")
+        def predict(c, half, into):
+            codes, plane = h[half]
+            rows = slice(c * P, (c + 1) * P)
+            y_sum = psum_y.tile([P, HALF], F32, name="y_bank")
             nc.tensor.matmul_mx(
                 out=y_sum[:],
-                lhsT=w2_codes[:, cols].bitcast(E4M3),
-                lhsT_scale=w2_plane[:, cols],
+                lhsT=w2_codes[:, rows].bitcast(E4M3),
+                lhsT_scale=w2_plane[:, rows],
                 rhs=codes[:].bitcast(E4M3),
                 rhs_scale=plane[:],
                 start=True,
@@ -216,36 +249,49 @@ def tile_list_cine_line_refill_kernel(
         def store(c):
             nc.sync.dma_start(out[c * P : (c + 1) * P, :], lines[c][:])
 
-        for c in range(LEAD):
-            gather_lines(c)
-        h = []
-        for half in range(HALVES):
-            cols = slice(half * HALF, (half + 1) * HALF)
-            h.append(coefficients(half))
-            if half == 0:
-                w2_early_rounded = shared.tile([P, EARLY_COLS * PACK], BF16, name="w2_early_rounded", offset=2048, align_bytes=64)
-                quantise_w2(w2_early, w2_early_rounded, 0, 0, EARLY_COLS)
-            gather_lines(LEAD + half)
-            if half == 0:
-                rest = shared.tile([P, ROW_TILES], F32, name="rest", offset=4096, align_bytes=64)
-                nc.scalar.activation(rest[:], weight, COPY, scale=-1.0, bias=1.0)
+        def refill_early(half):
             for c in range(EARLY_TILES):
                 if half == 0:
                     weigh_held(c)
-                moved = keep.tile([P, HALF], F32, name=f"moved_early{c}{half}")
-                predict(c, h[half], moved[:])
-                nc.vector.tensor_tensor(lines[c][:].indirect(list_half(half)), held[c][:, cols], moved[:], ADD)
+                moved = kept([P, HALF], F32, f"moved_early{c}{half}")
+                predict(c, half, moved[:])
+                nc.vector.tensor_tensor(lines[c][:].indirect(list_half(half)), held[c][:, entries(half)], moved[:], ADD)
                 if half == HALVES - 1:
                     store(c)
-        w2_late_rounded = shared.tile([P, (N - EARLY_COLS) * PACK], BF16, name="w2_late_rounded", offset=4160, align_bytes=64)
-        quantise_w2(w2_late, w2_late_rounded, 0, EARLY_COLS, 256)
-        quantise_w2(w2_late, w2_late_rounded, 256, 512, 512)
+
+        for c in range(LEAD):
+            gather_lines(c)
+        grouped = make_h(0, kept([P, PACK, HALF], BF16, "h_rounded0"))
+        quantise_w2(w2_early[:], 0, EARLY_COLS, "w2_grouped_early", after="h_rounded0")
+        h = [quantise_h(0, grouped, after="h_rounded0")]
+        gather_lines(LEAD, after="h_grouped0")
+        lam_turned = turn(lam_rows)
+        rest = kept([P, ROW_TILES], F32, "rest")
+        nc.scalar.activation(rest[:], lam_turned[:, 0:ROW_TILES], COPY, scale=-1.0, bias=1.0)
+        weight = kept([P, ROW_TILES], F32, "weight")
+        nc.scalar.copy(weight[:], lam_turned[:, 0:ROW_TILES])
+        refill_early(0)
+
+        grouped = make_h(1, placed([P, PACK, HALF], BF16, "h_rounded1", H_ROUNDED1_AT))
+        load_lines(ROW_TILES - 1)
+        w2_late = load_w2("w2_late", W2_LATE_AT, EARLY_COLS, N - EARLY_COLS)
+        h.append(quantise_h(1, grouped))
+        gather_lines(LEAD + 1, after="h_grouped1")
+        refill_early(1)
+
+        gather_lines(ROW_TILES - 1)
+        first = EARLY_COLS
+        for part_number, width in enumerate(LATE_WIDTHS):
+            after = f"moved_early{part_number}{HALVES - 1}"
+            slots = w2_late[:, :, first - EARLY_COLS : first - EARLY_COLS + width]
+            quantise_w2(slots, first, width, f"w2_grouped_late{part_number}", after)
+            gather_lines(LEAD + 2 + part_number, after)
+            first = first + width
+
         for c in range(EARLY_TILES, ROW_TILES):
-            if c + LEAD < ROW_TILES:
-                gather_lines(c + LEAD)
             weigh_held(c)
             moved = ring.tile([P, S], F32, name="moved")
             for half in range(HALVES):
-                predict(c, h[half], moved[:, half * HALF : (half + 1) * HALF])
+                predict(c, half, moved[:, entries(half)])
             nc.vector.tensor_tensor(lines[c][:].indirect(offsets[:]), held[c][:], moved[:], ADD)
             store(c)

@@ -28,7 +28,7 @@ HALVES = S // HALF
 LIST_COLS = HALF // 16
 ROW_TILES = N // P
 ALIGN = 64
-PARKED = 72
+MOVED_ROWS = 112
 EARLY_TILES = 2
 EARLY_COLS = EARLY_TILES * P
 LEAD = 3
@@ -36,24 +36,12 @@ LATE_WIDTHS = (256, 512)
 MOVED_BUFS = 4
 BANKS = 4
 
-LINE_BYTES = 4 * T
-LINES1_AT = 0
-SCALE_WINDOW_AT = LINES1_AT + LINE_BYTES - ALIGN
-LINES2_AT = SCALE_WINDOW_AT + T - ALIGN
-LINES3_AT = LINES2_AT + LINE_BYTES
-WINDOW0_AT = LINES3_AT + LINE_BYTES - ALIGN
-LINES4_AT = WINDOW0_AT + 4 * T - ALIGN
-LINES5_AT = LINES4_AT + LINE_BYTES
-WINDOW1_AT = LINES5_AT + LINE_BYTES - ALIGN
-LINES6_AT = WINDOW1_AT + 4 * T - ALIGN
-LINES7_AT = LINES6_AT + LINE_BYTES
-LAST_CODES_AT = LINES7_AT + LINE_BYTES - ALIGN
-W2_LATE_AT = LAST_CODES_AT + 4 * HALF - ALIGN
-LINES_AT = (None, LINES1_AT, LINES2_AT, LINES3_AT, LINES4_AT, LINES5_AT, LINES6_AT, LINES7_AT)
-W1_PLANES_AT = WINDOW0_AT + ALIGN
-W2_EARLY_AT = W1_PLANES_AT + PASSES * H
-LAM_ROWS_AT = W2_EARLY_AT + 4 * PACK * EARLY_COLS
-H_ROUNDED1_AT = LAM_ROWS_AT + 4 * P - 2 * PACK * HALF
+HELD_BYTES = 4 * S
+HELD_LEAD_AT = 0
+W2_EARLY_AT = HELD_LEAD_AT + HELD_BYTES - ALIGN
+REST_AT = W2_EARLY_AT + ALIGN
+H_CODES0_AT = REST_AT + ALIGN
+H_ROUNDED1_AT = W2_EARLY_AT + 4 * PACK * EARLY_COLS - ALIGN
 
 
 def tile_list_cine_line_refill_kernel(
@@ -74,33 +62,31 @@ def tile_list_cine_line_refill_kernel(
             return keep.tile(shape, dtype, name=name, tag=after or name, align_bytes=ALIGN)
 
         offsets = keep.tile([P, S // 16], U16, name="offsets")
-        scale_window = placed([P, T], U8, "scale_window", SCALE_WINDOW_AT)
+        scale_window = kept([P, T], U8, "scale_window")
         w1_scales_raw = kept([P, PASSES * H], U8, "w1_scales_raw")
         v_plane1 = kept([P, S], U8, "v_plane1")
-        bias_rows = kept([P, P], F32, "bias_rows")
+        vector_rows = kept([P, P], F32, "vector_rows")
         nc.vector.memset(scale_window[:].bitcast(I32), 0)
-        nc.gpsimd.memset(w1_scales_raw[:].bitcast(I32), 0)
+        nc.vector.memset(w1_scales_raw[:].bitcast(I32), 0)
         nc.vector.memset(v_plane1[:].bitcast(I32), 0)
-        nc.vector.memset(bias_rows[:], 0.0)
+        nc.vector.memset(vector_rows[:], 0.0)
 
         nc.sync.dma_start(offsets[:], offs)
-        w1_raw = kept([P, PASSES, 2 * H], U8, "w1_raw")
-        nc.sync.dma_start(w1_raw[:].bitcast(I32), w1_words.rearrange("a p c -> p a c").bitcast(I32))
         for q in range(QUADRANTS):
             nc.sync.dma_start(
-                scale_window[32 * q : 32 * q + PACK, :].bitcast(I32),
-                tab_scales[0, PACK * q : PACK * (q + 1), :].bitcast(I32),
+                scale_window[32 * q : 32 * q + PASSES * PACK, :].bitcast(I32),
+                tab_scales[:, PACK * q : PACK * (q + 1), :].bitcast(I32),
             )
-        nc.sync.dma_start(scale_window[PARKED : PARKED + PACK * QUADRANTS, :].bitcast(I32), tab_scales[1].bitcast(I32))
-        word_windows = [placed([P, T], U32, f"word_window{a}", (WINDOW0_AT, WINDOW1_AT)[a]) for a in range(PASSES)]
+        w1_raw = kept([P, PASSES, 2 * H], U8, "w1_raw")
+        nc.sync.dma_start(w1_raw[:].bitcast(I32), w1_words.rearrange("a p c -> p a c").bitcast(I32))
+        word_windows = [kept([P, T], U32, f"word_window{a}") for a in range(PASSES)]
         lines = {}
 
         def load_words(a):
             nc.sync.dma_start(word_windows[a][:].bitcast(I32), tab_words[a].rearrange("p t i -> p (t i)").bitcast(I32))
 
         def load_lines(c):
-            name = f"lines{c}"
-            lines[c] = kept([P, T], F32, name) if LINES_AT[c] is None else placed([P, T], F32, name, LINES_AT[c])
+            lines[c] = kept([P, T], F32, f"lines{c}")
             nc.sync.dma_start(lines[c][:], gT[c * P : (c + 1) * P, :])
 
         load_words(0)
@@ -110,22 +96,41 @@ def tile_list_cine_line_refill_kernel(
                 w1_scales[:, PACK * q : PACK * (q + 1), :].rearrange("a i c -> i a c").bitcast(I32),
             )
         load_words(1)
-        load_lines(0)
         nc.sync.dma_start(
-            bias_rows[0:PACK, :].rearrange("t (b j) -> t b j", j=RUN),
+            vector_rows[0:PACK, :].rearrange("t (b j) -> t b j", j=RUN),
             b1.rearrange("(b t j) -> t b j", t=PACK, j=RUN),
         )
+        load_lines(0)
+        nc.sync.dma_start(vector_rows[PACK : PACK + ROW_TILES, :], lam.rearrange("(c p) -> c p", p=P))
+
+        w2_rows = w2.rearrange("(b t j) n -> t b j n", t=PACK, j=RUN)
+
+        def load_w2(raw, first, width):
+            for t in range(PACK):
+                nc.sync.dma_start(raw[:, t, :], w2_rows[t, :, :, first : first + width])
+            return raw
+
+        for c in range(1, LEAD):
+            load_lines(c)
+        w2_early = load_w2(placed([P, PACK, EARLY_COLS], F32, "w2_early", W2_EARLY_AT), 0, EARLY_COLS)
+        for c in range(LEAD, LEAD + 2):
+            load_lines(c)
+        w2_late = []
+        first = EARLY_COLS
+        for part_number, width in enumerate(LATE_WIDTHS):
+            w2_late.append(load_w2(kept([P, PACK, width], F32, f"w2_late{part_number}"), first, width))
+            first = first + width
+        for c in range(LEAD + 2, ROW_TILES):
+            load_lines(c)
 
         identity = kept([P, P], F32, "identity")
         make_identity(nc, identity[:])
-
-        def turn(rows):
-            turned = psum_y.tile([P, HALF], F32, name="y_bank")
-            nc.tensor.transpose(turned[:, 0:P], rows[:], identity[:])
-            return turned
-
-        bias = kept([P, PACK], F32, "bias")
-        nc.scalar.copy(bias[:], turn(bias_rows)[:, 0:PACK])
+        turned = psum_y.tile([P, HALF], F32, name="y_bank")
+        nc.tensor.transpose(turned[:, 0:P], vector_rows[:], identity[:])
+        vectors = kept([P, PACK + ROW_TILES], F32, "vectors")
+        nc.scalar.copy(vectors[:], turned[:, 0 : PACK + ROW_TILES])
+        bias = vectors[:, 0:PACK]
+        weight = vectors[:, PACK : PACK + ROW_TILES]
 
         def reorder_columns(into, raw, words):
             nc.vector.tensor_copy(
@@ -133,17 +138,15 @@ def tile_list_cine_line_refill_kernel(
                 raw.bitcast(I32).rearrange("p (a b t w) -> p a t b w", a=PASSES, t=PACK, w=words),
             )
 
-        w1_codes = kept([P, PASSES * 2 * H], U8, "w1_codes")
-        reorder_columns(w1_codes[:], w1_raw[:].rearrange("p a c -> p (a c)"), 2 * RUN // 4)
-
         v_plane0 = kept([P, S], U8, "v_plane0")
         nc.vector.tensor_copy(v_plane0[:], scale_window[:].indirect(offsets[:]))
-        for q in range(QUADRANTS):
-            nc.sync.dma_start(
-                v_plane1[32 * q : 32 * q + PACK, :].bitcast(I32),
-                v_plane0[PARKED + PACK * q : PARKED + PACK * (q + 1), :].bitcast(I32),
-            )
+        nc.scalar.dma_start(
+            v_plane1[0:MOVED_ROWS, :].bitcast(I32), v_plane0[PACK : PACK + MOVED_ROWS, :].bitcast(I32)
+        )
         v_planes = [v_plane0, v_plane1]
+
+        w1_codes = kept([P, PASSES * 2 * H], U8, "w1_codes")
+        reorder_columns(w1_codes[:], w1_raw[:].rearrange("p a c -> p (a c)"), 2 * RUN // 4)
 
         def list_half(half):
             return offsets[:, half * LIST_COLS : (half + 1) * LIST_COLS]
@@ -153,29 +156,11 @@ def tile_list_cine_line_refill_kernel(
 
         v_codes0 = kept([P, S], U32, "v_codes0")
         nc.vector.tensor_copy(v_codes0[:], word_windows[0][:].indirect(offsets[:]))
-        w1_planes = placed([P, PASSES * H], U8, "w1_planes", W1_PLANES_AT)
+        w1_planes = kept([P, PASSES * H], U8, "w1_planes")
         reorder_columns(w1_planes[:], w1_scales_raw[:], RUN // 4)
-        v_codes1 = [kept([P, HALF], U32, "v_codes1_first"), placed([P, HALF], U32, "v_codes1_last", LAST_CODES_AT)]
+        v_codes1 = [kept([P, HALF], U32, f"v_codes1_{half}") for half in range(HALVES)]
         for half in range(HALVES):
             nc.vector.tensor_copy(v_codes1[half][:], word_windows[1][:].indirect(list_half(half)))
-
-        w2_rows = w2.rearrange("(b t j) n -> t b j n", t=PACK, j=RUN)
-
-        def load_w2(name, at, first, width):
-            raw = placed([P, PACK, width], F32, name, at)
-            for t in range(PACK):
-                nc.sync.dma_start(raw[:, t, :], w2_rows[t, :, :, first : first + width])
-            return raw
-
-        for c in range(1, LEAD):
-            load_lines(c)
-        w2_early = load_w2("w2_early", W2_EARLY_AT, 0, EARLY_COLS)
-        load_lines(LEAD)
-        lam_rows = placed([P, P], F32, "lam_rows", LAM_ROWS_AT)
-        nc.gpsimd.memset(lam_rows[:], 0.0)
-        nc.sync.dma_start(lam_rows[0:ROW_TILES, :], lam.rearrange("(c p) -> c p", p=P))
-        for c in range(LEAD + 1, ROW_TILES - 1):
-            load_lines(c)
 
         def interleave(grouped, slots):
             nc.scalar.copy(
@@ -186,9 +171,9 @@ def tile_list_cine_line_refill_kernel(
         w2_codes = kept([P, N], U32, "w2_codes")
         w2_plane = kept([P, N], U8, "w2_plane")
 
-        def quantise_w2(slots, first, width, name, after):
-            grouped = kept([P, width * PACK], BF16, name, after)
-            interleave(grouped, slots)
+        def quantise_w2(raw, first, width):
+            grouped = kept([P, width * PACK], BF16, f"w2_grouped{first}")
+            interleave(grouped, raw[:])
             nc.vector.quantize_mx(
                 out=w2_codes[:, first : first + width].bitcast(E4M3),
                 scales=w2_plane[:, first : first + width],
@@ -216,17 +201,19 @@ def tile_list_cine_line_refill_kernel(
             interleave(grouped, rounded[:])
             return grouped
 
-        def quantise_h(half, grouped, after=None):
-            codes = kept([P, HALF], U32, f"h_codes{half}", after)
+        def quantise_h(half, grouped, codes):
             plane = kept([P, HALF], U8, f"h_plane{half}")
             nc.vector.quantize_mx(out=codes[:].bitcast(E4M3), scales=plane[:], in_=grouped[:])
             return codes, plane
 
         held = {}
 
-        def gather_lines(c, after=None):
-            held[c] = kept([P, S], F32, f"held{c}", after)
-            nc.vector.tensor_copy(held[c][:], lines[c][:].indirect(offsets[:]))
+        def gather_lines(c, into):
+            held[c] = into
+            nc.vector.tensor_copy(into[:], lines[c][:].indirect(offsets[:]))
+
+        def own_held(c, after=None):
+            return kept([P, S], F32, f"held{c}", after)
 
         def weigh_held(c):
             nc.scalar.activation(held[c][:], held[c][:], COPY, scale=rest[:, c : c + 1])
@@ -260,33 +247,27 @@ def tile_list_cine_line_refill_kernel(
                     store(c)
 
         for c in range(LEAD):
-            gather_lines(c)
+            gather_lines(c, own_held(c))
         grouped = make_h(0, kept([P, PACK, HALF], BF16, "h_rounded0"))
-        quantise_w2(w2_early[:], 0, EARLY_COLS, "w2_grouped_early", after="h_rounded0")
-        h = [quantise_h(0, grouped, after="h_rounded0")]
-        gather_lines(LEAD, after="h_grouped0")
-        lam_turned = turn(lam_rows)
-        rest = kept([P, ROW_TILES], F32, "rest")
-        nc.scalar.activation(rest[:], lam_turned[:, 0:ROW_TILES], COPY, scale=-1.0, bias=1.0)
-        weight = kept([P, ROW_TILES], F32, "weight")
-        nc.scalar.copy(weight[:], lam_turned[:, 0:ROW_TILES])
+        quantise_w2(w2_early, 0, EARLY_COLS)
+        h = [quantise_h(0, grouped, placed([P, HALF], U32, "h_codes0", H_CODES0_AT))]
+        gather_lines(LEAD, placed([P, S], F32, "held_lead", HELD_LEAD_AT))
+        rest = placed([P, ROW_TILES], F32, "rest", REST_AT)
+        nc.scalar.activation(rest[:], weight, COPY, scale=-1.0, bias=1.0)
         refill_early(0)
 
         grouped = make_h(1, placed([P, PACK, HALF], BF16, "h_rounded1", H_ROUNDED1_AT))
-        load_lines(ROW_TILES - 1)
-        w2_late = load_w2("w2_late", W2_LATE_AT, EARLY_COLS, N - EARLY_COLS)
-        h.append(quantise_h(1, grouped))
-        gather_lines(LEAD + 1, after="h_grouped1")
+        h.append(quantise_h(1, grouped, kept([P, HALF], U32, "h_codes1")))
+        gather_lines(LEAD + 1, placed([P, S], F32, "held_next", H_ROUNDED1_AT))
         refill_early(1)
 
-        gather_lines(ROW_TILES - 1)
         first = EARLY_COLS
         for part_number, width in enumerate(LATE_WIDTHS):
-            after = f"moved_early{part_number}{HALVES - 1}"
-            slots = w2_late[:, :, first - EARLY_COLS : first - EARLY_COLS + width]
-            quantise_w2(slots, first, width, f"w2_grouped_late{part_number}", after)
-            gather_lines(LEAD + 2 + part_number, after)
+            quantise_w2(w2_late[part_number], first, width)
+            c = LEAD + 2 + part_number
+            gather_lines(c, own_held(c, f"w2_late{part_number}"))
             first = first + width
+        gather_lines(ROW_TILES - 1, own_held(ROW_TILES - 1))
 
         for c in range(EARLY_TILES, ROW_TILES):
             weigh_held(c)

@@ -28,7 +28,7 @@ HALVES = S // HALF
 LIST_COLS = HALF // 16
 ROW_TILES = N // P
 ALIGN = 64
-MOVED_ROWS = 112
+PARKED = 72
 EARLY_TILES = 2
 EARLY_COLS = EARLY_TILES * P
 LEAD = 3
@@ -74,9 +74,10 @@ def tile_list_cine_line_refill_kernel(
         nc.sync.dma_start(offsets[:], offs)
         for q in range(QUADRANTS):
             nc.sync.dma_start(
-                scale_window[32 * q : 32 * q + PASSES * PACK, :].bitcast(I32),
-                tab_scales[:, PACK * q : PACK * (q + 1), :].bitcast(I32),
+                scale_window[32 * q : 32 * q + PACK, :].bitcast(I32),
+                tab_scales[0, PACK * q : PACK * (q + 1), :].bitcast(I32),
             )
+        nc.sync.dma_start(scale_window[PARKED : PARKED + PACK * QUADRANTS, :].bitcast(I32), tab_scales[1].bitcast(I32))
         w1_raw = kept([P, PASSES, 2 * H], U8, "w1_raw")
         nc.sync.dma_start(w1_raw[:].bitcast(I32), w1_words.rearrange("a p c -> p a c").bitcast(I32))
         word_windows = [kept([P, T], U32, f"word_window{a}") for a in range(PASSES)]
@@ -100,8 +101,18 @@ def tile_list_cine_line_refill_kernel(
             vector_rows[0:PACK, :].rearrange("t (b j) -> t b j", j=RUN),
             b1.rearrange("(b t j) -> t b j", t=PACK, j=RUN),
         )
-        load_lines(0)
         nc.sync.dma_start(vector_rows[PACK : PACK + ROW_TILES, :], lam.rearrange("(c p) -> c p", p=P))
+
+        v_plane0 = kept([P, S], U8, "v_plane0")
+        nc.vector.tensor_copy(v_plane0[:], scale_window[:].indirect(offsets[:]))
+        for q in range(QUADRANTS):
+            nc.sync.dma_start(
+                v_plane1[32 * q : 32 * q + PACK, :].bitcast(I32),
+                v_plane0[PARKED + PACK * q : PARKED + PACK * (q + 1), :].bitcast(I32),
+            )
+        v_planes = [v_plane0, v_plane1]
+
+        load_lines(0)
 
         w2_rows = w2.rearrange("(b t j) n -> t b j n", t=PACK, j=RUN)
 
@@ -138,13 +149,6 @@ def tile_list_cine_line_refill_kernel(
                 raw.bitcast(I32).rearrange("p (a b t w) -> p a t b w", a=PASSES, t=PACK, w=words),
             )
 
-        v_plane0 = kept([P, S], U8, "v_plane0")
-        nc.vector.tensor_copy(v_plane0[:], scale_window[:].indirect(offsets[:]))
-        nc.scalar.dma_start(
-            v_plane1[0:MOVED_ROWS, :].bitcast(I32), v_plane0[PACK : PACK + MOVED_ROWS, :].bitcast(I32)
-        )
-        v_planes = [v_plane0, v_plane1]
-
         w1_codes = kept([P, PASSES * 2 * H], U8, "w1_codes")
         reorder_columns(w1_codes[:], w1_raw[:].rearrange("p a c -> p (a c)"), 2 * RUN // 4)
 
@@ -171,8 +175,8 @@ def tile_list_cine_line_refill_kernel(
         w2_codes = kept([P, N], U32, "w2_codes")
         w2_plane = kept([P, N], U8, "w2_plane")
 
-        def quantise_w2(raw, first, width):
-            grouped = kept([P, width * PACK], BF16, f"w2_grouped{first}")
+        def quantise_w2(raw, first, width, after=None):
+            grouped = kept([P, width * PACK], BF16, f"w2_grouped{first}", after)
             interleave(grouped, raw[:])
             nc.vector.quantize_mx(
                 out=w2_codes[:, first : first + width].bitcast(E4M3),
@@ -249,7 +253,7 @@ def tile_list_cine_line_refill_kernel(
         for c in range(LEAD):
             gather_lines(c, own_held(c))
         grouped = make_h(0, kept([P, PACK, HALF], BF16, "h_rounded0"))
-        quantise_w2(w2_early, 0, EARLY_COLS)
+        quantise_w2(w2_early, 0, EARLY_COLS, after="h_rounded0")
         h = [quantise_h(0, grouped, placed([P, HALF], U32, "h_codes0", H_CODES0_AT))]
         gather_lines(LEAD, placed([P, S], F32, "held_lead", HELD_LEAD_AT))
         rest = placed([P, ROW_TILES], F32, "rest", REST_AT)

@@ -219,8 +219,8 @@ def tile_list_cine_line_refill_kernel(
         def own_held(c, after=None):
             return kept([P, S], F32, f"held{c}", after)
 
-        def weigh_held(c):
-            nc.scalar.activation(held[c][:], held[c][:], COPY, scale=rest[:, c : c + 1])
+        def weigh_held(c, columns):
+            nc.scalar.activation(held[c][:, columns], held[c][:, columns], COPY, scale=rest[:, c : c + 1])
 
         def predict(c, half, into):
             codes, plane = h[half]
@@ -242,8 +242,7 @@ def tile_list_cine_line_refill_kernel(
 
         def refill_early(half):
             for c in range(EARLY_TILES):
-                if half == 0:
-                    weigh_held(c)
+                weigh_held(c, entries(half))
                 moved = kept([P, HALF], F32, f"moved_early{c}{half}")
                 predict(c, half, moved[:])
                 nc.vector.tensor_tensor(lines[c][:].indirect(list_half(half)), held[c][:, entries(half)], moved[:], ADD)
@@ -274,7 +273,7 @@ def tile_list_cine_line_refill_kernel(
         gather_lines(ROW_TILES - 1, own_held(ROW_TILES - 1))
 
         for c in range(EARLY_TILES, ROW_TILES):
-            weigh_held(c)
+            weigh_held(c, slice(0, S))
             moved = ring.tile([P, S], F32, name="moved")
             for half in range(HALVES):
                 predict(c, half, moved[:, entries(half)])

@@ -28,20 +28,18 @@ HALVES = S // HALF
 LIST_COLS = HALF // 16
 ROW_TILES = N // P
 ALIGN = 64
-PARKED = 72
-EARLY_TILES = 2
-EARLY_COLS = EARLY_TILES * P
+PARKED = 16
 LEAD = 3
-LATE_WIDTHS = (256, 512)
+W2_PARTS = (128, 128, 256, 512)
+AHEAD_BANKS = 2
 MOVED_BUFS = 4
 BANKS = 4
 
 HELD_BYTES = 4 * S
-HELD_LEAD_AT = 0
-W2_EARLY_AT = HELD_LEAD_AT + HELD_BYTES - ALIGN
-REST_AT = W2_EARLY_AT + ALIGN
-H_CODES0_AT = REST_AT + ALIGN
-H_ROUNDED1_AT = W2_EARLY_AT + 4 * PACK * EARLY_COLS - ALIGN
+W2_FIRST_AT = HELD_BYTES - ALIGN
+H_ROUNDED1_AT = W2_FIRST_AT + 4 * PACK * W2_PARTS[0] - ALIGN
+W2_SECOND_AT = H_ROUNDED1_AT + 2 * PACK * HALF + HELD_BYTES - ALIGN
+W2_AT = (W2_FIRST_AT, W2_SECOND_AT)
 
 
 def tile_list_cine_line_refill_kernel(
@@ -64,20 +62,15 @@ def tile_list_cine_line_refill_kernel(
         offsets = keep.tile([P, S // 16], U16, name="offsets")
         scale_window = kept([P, T], U8, "scale_window")
         w1_scales_raw = kept([P, PASSES * H], U8, "w1_scales_raw")
-        v_plane1 = kept([P, S], U8, "v_plane1")
         vector_rows = kept([P, P], F32, "vector_rows")
-        nc.vector.memset(scale_window[:].bitcast(I32), 0)
+        nc.gpsimd.memset(scale_window[:].bitcast(I32), 0)
         nc.vector.memset(w1_scales_raw[:].bitcast(I32), 0)
-        nc.vector.memset(v_plane1[:].bitcast(I32), 0)
         nc.vector.memset(vector_rows[:], 0.0)
 
         nc.sync.dma_start(offsets[:], offs)
-        for q in range(QUADRANTS):
-            nc.sync.dma_start(
-                scale_window[32 * q : 32 * q + PACK, :].bitcast(I32),
-                tab_scales[0, PACK * q : PACK * (q + 1), :].bitcast(I32),
-            )
-        nc.sync.dma_start(scale_window[PARKED : PARKED + PACK * QUADRANTS, :].bitcast(I32), tab_scales[1].bitcast(I32))
+        tab_rows = tab_scales.rearrange("a (q r) t -> r q a t", r=PACK)
+        for r in range(PACK):
+            nc.sync.dma_start(scale_window[r:P:PARKED, :].bitcast(I32), tab_rows[r].bitcast(I32))
         w1_raw = kept([P, PASSES, 2 * H], U8, "w1_raw")
         nc.sync.dma_start(w1_raw[:].bitcast(I32), w1_words.rearrange("a p c -> p a c").bitcast(I32))
         word_windows = [kept([P, T], U32, f"word_window{a}") for a in range(PASSES)]
@@ -91,10 +84,11 @@ def tile_list_cine_line_refill_kernel(
             nc.sync.dma_start(lines[c][:], gT[c * P : (c + 1) * P, :])
 
         load_words(0)
-        for q in range(QUADRANTS):
+        w1_rows = w1_scales.rearrange("a (q r) c -> r q a c", r=PACK)
+        for r in range(PACK):
             nc.sync.dma_start(
-                w1_scales_raw[32 * q : 32 * q + PACK, :].rearrange("i (a c) -> i a c", a=PASSES).bitcast(I32),
-                w1_scales[:, PACK * q : PACK * (q + 1), :].rearrange("a i c -> i a c").bitcast(I32),
+                w1_scales_raw[r:P:32, :].rearrange("q (a c) -> q a c", a=PASSES).bitcast(I32),
+                w1_rows[r].bitcast(I32),
             )
         load_words(1)
         nc.sync.dma_start(
@@ -104,35 +98,33 @@ def tile_list_cine_line_refill_kernel(
         nc.sync.dma_start(vector_rows[PACK : PACK + ROW_TILES, :], lam.rearrange("(c p) -> c p", p=P))
 
         v_plane0 = kept([P, S], U8, "v_plane0")
+        v_plane1 = kept([P, S], U8, "v_plane1")
         nc.vector.tensor_copy(v_plane0[:], scale_window[:].indirect(offsets[:]))
-        for q in range(QUADRANTS):
-            nc.sync.dma_start(
-                v_plane1[32 * q : 32 * q + PACK, :].bitcast(I32),
-                v_plane0[PARKED + PACK * q : PARKED + PACK * (q + 1), :].bitcast(I32),
-            )
+        for r in range(PACK):
+            nc.sync.dma_start(v_plane1[r:P:32, :].bitcast(I32), v_plane0[PARKED + r : P : 32, :].bitcast(I32))
         v_planes = [v_plane0, v_plane1]
 
-        load_lines(0)
-
         w2_rows = w2.rearrange("(b t j) n -> t b j n", t=PACK, j=RUN)
+        w2_raw = [placed([P, PACK, W2_PARTS[part]], F32, f"w2_raw{part}", W2_AT[part]) for part in range(HALVES)]
+        for part in range(HALVES, len(W2_PARTS)):
+            w2_raw.append(kept([P, PACK, W2_PARTS[part]], F32, f"w2_raw{part}"))
 
-        def load_w2(raw, first, width):
+        def w2_columns(part):
+            first = sum(W2_PARTS[:part])
+            return slice(first, first + W2_PARTS[part])
+
+        def load_w2(part):
             for t in range(PACK):
-                nc.sync.dma_start(raw[:, t, :], w2_rows[t, :, :, first : first + width])
-            return raw
+                nc.sync.dma_start(w2_raw[part][:, t, :], w2_rows[t, :, :, w2_columns(part)])
 
-        for c in range(1, LEAD):
+        for c in range(LEAD):
             load_lines(c)
-        w2_early = load_w2(placed([P, PACK, EARLY_COLS], F32, "w2_early", W2_EARLY_AT), 0, EARLY_COLS)
-        for c in range(LEAD, LEAD + 2):
-            load_lines(c)
-        w2_late = []
-        first = EARLY_COLS
-        for part_number, width in enumerate(LATE_WIDTHS):
-            w2_late.append(load_w2(kept([P, PACK, width], F32, f"w2_late{part_number}"), first, width))
-            first = first + width
-        for c in range(LEAD + 2, ROW_TILES):
-            load_lines(c)
+        load_w2(0)
+        load_lines(LEAD)
+        load_lines(LEAD + 1)
+        for part in range(1, len(W2_PARTS)):
+            load_lines(LEAD + 1 + part)
+            load_w2(part)
 
         identity = kept([P, P], F32, "identity")
         make_identity(nc, identity[:])
@@ -175,20 +167,18 @@ def tile_list_cine_line_refill_kernel(
         w2_codes = kept([P, N], U32, "w2_codes")
         w2_plane = kept([P, N], U8, "w2_plane")
 
-        def quantise_w2(raw, first, width, after=None):
-            grouped = kept([P, width * PACK], BF16, f"w2_grouped{first}", after)
-            interleave(grouped, raw[:])
-            nc.vector.quantize_mx(
-                out=w2_codes[:, first : first + width].bitcast(E4M3),
-                scales=w2_plane[:, first : first + width],
-                in_=grouped[:],
-            )
+        def quantise_w2(part, after=None):
+            grouped = kept([P, W2_PARTS[part] * PACK], BF16, f"w2_grouped{part}", after)
+            interleave(grouped, w2_raw[part][:])
+            columns = w2_columns(part)
+            nc.vector.quantize_mx(out=w2_codes[:, columns].bitcast(E4M3), scales=w2_plane[:, columns], in_=grouped[:])
 
         def make_h(half, rounded):
             sums = [psum_h.tile([P, HALF], F32, name="h_bank") for t in range(PACK)]
             moving = [v_codes0[:, entries(half)], v_codes1[half][:]]
-            for a in range(PASSES):
-                for t in range(PACK):
+            for t in range(PACK):
+                passes = (0, 1) if t < AHEAD_BANKS else (1, 0)
+                for a in passes:
                     first = a * H + t * P
                     nc.tensor.matmul_mx(
                         out=sums[t][:],
@@ -196,8 +186,8 @@ def tile_list_cine_line_refill_kernel(
                         lhsT_scale=w1_planes[:, first : first + P],
                         rhs=moving[a].bitcast(E4M3),
                         rhs_scale=v_planes[a][:, entries(half)],
-                        start=(a == 0),
-                        stop=(a == PASSES - 1),
+                        start=(a == passes[0]),
+                        stop=(a == passes[-1]),
                     )
             for t in range(PACK):
                 nc.scalar.activation(rounded[:, t, :], sums[t][:], IDENTITY, bias=bias[:, t : t + 1])
@@ -205,8 +195,8 @@ def tile_list_cine_line_refill_kernel(
             interleave(grouped, rounded[:])
             return grouped
 
-        def quantise_h(half, grouped, codes):
-            plane = kept([P, HALF], U8, f"h_plane{half}")
+        def quantise_h(half, grouped, plane):
+            codes = kept([P, HALF], U32, f"h_codes{half}")
             nc.vector.quantize_mx(out=codes[:].bitcast(E4M3), scales=plane[:], in_=grouped[:])
             return codes, plane
 
@@ -220,7 +210,7 @@ def tile_list_cine_line_refill_kernel(
             return kept([P, S], F32, f"held{c}", after)
 
         def weigh_held(c, columns):
-            nc.scalar.activation(held[c][:, columns], held[c][:, columns], COPY, scale=rest[:, c : c + 1])
+            nc.scalar.activation(held[c][:, columns], held[c][:, columns], COPY, scale=rest[c])
 
         def predict(c, half, into):
             codes, plane = h[half]
@@ -240,42 +230,54 @@ def tile_list_cine_line_refill_kernel(
         def store(c):
             nc.sync.dma_start(out[c * P : (c + 1) * P, :], lines[c][:])
 
-        def refill_early(half):
-            for c in range(EARLY_TILES):
-                weigh_held(c, entries(half))
-                moved = kept([P, HALF], F32, f"moved_early{c}{half}")
-                predict(c, half, moved[:])
-                nc.vector.tensor_tensor(lines[c][:].indirect(list_half(half)), held[c][:, entries(half)], moved[:], ADD)
-                if half == HALVES - 1:
-                    store(c)
+        rest = {}
 
-        for c in range(LEAD):
-            gather_lines(c, own_held(c))
-        grouped = make_h(0, kept([P, PACK, HALF], BF16, "h_rounded0"))
-        quantise_w2(w2_early, 0, EARLY_COLS, after="h_rounded0")
-        h = [quantise_h(0, grouped, placed([P, HALF], U32, "h_codes0", H_CODES0_AT))]
-        gather_lines(LEAD, placed([P, S], F32, "held_lead", HELD_LEAD_AT))
-        rest = placed([P, ROW_TILES], F32, "rest", REST_AT)
-        nc.scalar.activation(rest[:], weight, COPY, scale=-1.0, bias=1.0)
-        refill_early(0)
+        def complement(tiles, name, at):
+            columns = placed([P, len(tiles)], F32, name, at)
+            nc.scalar.activation(columns[:], weight[:, tiles.start : tiles.stop], COPY, scale=-1.0, bias=1.0)
+            for c in tiles:
+                rest[c] = columns[:, c - tiles.start : c - tiles.start + 1]
 
-        grouped = make_h(1, placed([P, PACK, HALF], BF16, "h_rounded1", H_ROUNDED1_AT))
-        h.append(quantise_h(1, grouped, kept([P, HALF], U32, "h_codes1")))
-        gather_lines(LEAD + 1, placed([P, S], F32, "held_next", H_ROUNDED1_AT))
-        refill_early(1)
+        def refill_half(half):
+            moved = kept([P, HALF], F32, f"moved_half{half}")
+            weigh_held(0, entries(half))
+            predict(0, half, moved[:])
+            nc.vector.tensor_tensor(lines[0][:].indirect(list_half(half)), held[0][:, entries(half)], moved[:], ADD)
 
-        first = EARLY_COLS
-        for part_number, width in enumerate(LATE_WIDTHS):
-            quantise_w2(w2_late[part_number], first, width)
-            c = LEAD + 2 + part_number
-            gather_lines(c, own_held(c, f"w2_late{part_number}"))
-            first = first + width
-        gather_lines(ROW_TILES - 1, own_held(ROW_TILES - 1))
-
-        for c in range(EARLY_TILES, ROW_TILES):
+        def refill(c):
             weigh_held(c, slice(0, S))
             moved = ring.tile([P, S], F32, name="moved")
             for half in range(HALVES):
                 predict(c, half, moved[:, entries(half)])
             nc.vector.tensor_tensor(lines[c][:].indirect(offsets[:]), held[c][:], moved[:], ADD)
             store(c)
+
+        def behind_w2(part, shape, dtype, name, past):
+            return placed(shape, dtype, name, W2_AT[part] + past)
+
+        for c in range(LEAD):
+            gather_lines(c, own_held(c))
+        grouped = make_h(0, kept([P, PACK, HALF], BF16, "h_rounded0"))
+        quantise_w2(0, after="h_rounded0")
+        h = [quantise_h(0, grouped, behind_w2(0, [P, HALF], U8, "h_plane0", 2 * ALIGN))]
+        gather_lines(LEAD, behind_w2(0, [P, S], F32, "held_first", ALIGN - HELD_BYTES))
+        complement(range(0, 1), "rest_first", W2_FIRST_AT + ALIGN)
+        refill_half(0)
+        gather_lines(LEAD + 1, own_held(LEAD + 1))
+
+        grouped = make_h(1, placed([P, PACK, HALF], BF16, "h_rounded1", H_ROUNDED1_AT))
+        h.append(quantise_h(1, grouped, behind_w2(1, [P, HALF], U8, "h_plane1", 2 * ALIGN)))
+        quantise_w2(1)
+        gather_lines(LEAD + 2, behind_w2(1, [P, S], F32, "held_second", ALIGN - HELD_BYTES))
+        complement(range(1, ROW_TILES), "rest_others", W2_SECOND_AT + ALIGN)
+        refill_half(1)
+        store(0)
+        refill(1)
+
+        for part in range(HALVES, len(W2_PARTS)):
+            quantise_w2(part)
+            c = LEAD + 1 + part
+            gather_lines(c, own_held(c, f"w2_raw{part}"))
+
+        for c in range(HALVES, ROW_TILES):
+            refill(c)

@@ -63,7 +63,7 @@ def tile_list_cine_line_refill_kernel(
         scale_window = kept([P, T], U8, "scale_window")
         w1_scales_raw = kept([P, PASSES * H], U8, "w1_scales_raw")
         vector_rows = kept([P, P], F32, "vector_rows")
-        nc.gpsimd.memset(scale_window[:].bitcast(I32), 0)
+        nc.vector.memset(scale_window[:].bitcast(I32), 0)
         nc.vector.memset(w1_scales_raw[:].bitcast(I32), 0)
         nc.vector.memset(vector_rows[:], 0.0)
 

@@ -68,11 +68,11 @@ def tile_list_cine_line_refill_kernel(
         nc.vector.memset(vector_rows[:], 0.0)
 
         nc.sync.dma_start(offsets[:], offs)
+        w1_raw = kept([P, PASSES, 2 * H], U8, "w1_raw")
+        nc.sync.dma_start(w1_raw[:].bitcast(I32), w1_words.rearrange("a p c -> p a c").bitcast(I32))
         tab_rows = tab_scales.rearrange("a (q r) t -> r q a t", r=PACK)
         for r in range(PACK):
             nc.sync.dma_start(scale_window[r:P:PARKED, :].bitcast(I32), tab_rows[r].bitcast(I32))
-        w1_raw = kept([P, PASSES, 2 * H], U8, "w1_raw")
-        nc.sync.dma_start(w1_raw[:].bitcast(I32), w1_words.rearrange("a p c -> p a c").bitcast(I32))
         word_windows = [kept([P, T], U32, f"word_window{a}") for a in range(PASSES)]
         lines = {}
 
@@ -136,9 +136,9 @@ def tile_list_cine_line_refill_kernel(
         weight = vectors[:, PACK : PACK + ROW_TILES]
 
         def reorder_columns(into, raw, words):
-            nc.vector.tensor_copy(
-                into.bitcast(I32).rearrange("p (a t b w) -> p a t b w", a=PASSES, t=PACK, w=words),
-                raw.bitcast(I32).rearrange("p (a b t w) -> p a t b w", a=PASSES, t=PACK, w=words),
+            nc.scalar.copy(
+                into.bitcast(U32).rearrange("p (a t b w) -> p a t b w", a=PASSES, t=PACK, w=words),
+                raw.bitcast(U32).rearrange("p (a b t w) -> p a t b w", a=PASSES, t=PACK, w=words),
             )
 
         w1_codes = kept([P, PASSES * 2 * H], U8, "w1_codes")

@@ -1,7 +1,6 @@
 from contextlib import ExitStack
 
 import concourse.mybir as mybir
-from concourse.masks import make_identity
 
 K, T, S, H, N = 1024, 2048, 1024, 512, 1024
 FLOPS = 2 * K * H * S + 2 * H * N * S
@@ -20,8 +19,8 @@ ADD = mybir.AluOpType.add
 
 P = 128
 PACK = 4
-QUADRANTS = 4
-RUN = 8
+PAIR = 2
+SPAN = PACK * PAIR
 PASSES = K // (P * PACK)
 HALF = 512
 HALVES = S // HALF
@@ -62,14 +61,12 @@ def tile_list_cine_line_refill_kernel(
         offsets = keep.tile([P, S // 16], U16, name="offsets")
         scale_window = kept([P, T], U8, "scale_window")
         w1_scales_raw = kept([P, PASSES * H], U8, "w1_scales_raw")
-        vector_rows = kept([P, P], F32, "vector_rows")
         nc.vector.memset(scale_window[:].bitcast(I32), 0)
         nc.vector.memset(w1_scales_raw[:].bitcast(I32), 0)
-        nc.vector.memset(vector_rows[:], 0.0)
 
-        nc.sync.dma_start(offsets[:], offs)
         w1_raw = kept([P, PASSES, 2 * H], U8, "w1_raw")
         nc.sync.dma_start(w1_raw[:].bitcast(I32), w1_words.rearrange("a p c -> p a c").bitcast(I32))
+        nc.sync.dma_start(offsets[:], offs)
         tab_rows = tab_scales.rearrange("a (q r) t -> r q a t", r=PACK)
         for r in range(PACK):
             nc.sync.dma_start(scale_window[r:P:PARKED, :].bitcast(I32), tab_rows[r].bitcast(I32))
@@ -91,11 +88,12 @@ def tile_list_cine_line_refill_kernel(
                 w1_rows[r].bitcast(I32),
             )
         load_words(1)
-        nc.sync.dma_start(
-            vector_rows[0:PACK, :].rearrange("t (b j) -> t b j", j=RUN),
-            b1.rearrange("(b t j) -> t b j", t=PACK, j=RUN),
-        )
-        nc.sync.dma_start(vector_rows[PACK : PACK + ROW_TILES, :], lam.rearrange("(c p) -> c p", p=P))
+
+        bias = kept([P, SPAN], F32, "bias")
+        for e in range(PAIR):
+            nc.sync.dma_start(
+                bias[e:P:PAIR, 0 : SPAN - 1], b1.rearrange("(m x) -> m x", x=SPAN)[:, e : e + SPAN - 1]
+            )
 
         v_plane0 = kept([P, S], U8, "v_plane0")
         v_plane1 = kept([P, S], U8, "v_plane1")
@@ -104,7 +102,7 @@ def tile_list_cine_line_refill_kernel(
             nc.sync.dma_start(v_plane1[r:P:32, :].bitcast(I32), v_plane0[PARKED + r : P : 32, :].bitcast(I32))
         v_planes = [v_plane0, v_plane1]
 
-        w2_rows = w2.rearrange("(b t j) n -> t b j n", t=PACK, j=RUN)
+        w2_rows = w2.rearrange("(m t e) n -> e m t n", t=PACK, e=PAIR)
         w2_raw = [placed([P, PACK, W2_PARTS[part]], F32, f"w2_raw{part}", W2_AT[part]) for part in range(HALVES)]
         for part in range(HALVES, len(W2_PARTS)):
             w2_raw.append(kept([P, PACK, W2_PARTS[part]], F32, f"w2_raw{part}"))
@@ -114,35 +112,40 @@ def tile_list_cine_line_refill_kernel(
             return slice(first, first + W2_PARTS[part])
 
         def load_w2(part):
-            for t in range(PACK):
-                nc.sync.dma_start(w2_raw[part][:, t, :], w2_rows[t, :, :, w2_columns(part)])
+            for e in range(PAIR):
+                nc.sync.dma_start(w2_raw[part][e:P:PAIR, :, :], w2_rows[e, :, :, w2_columns(part)])
+
+        weights = {}
+
+        def load_weights(tiles, name):
+            columns = kept([P, len(tiles)], F32, name)
+            with nc.allow_non_contiguous_dma(reason="one value for each partition"):
+                nc.sync.dma_start(columns[:], lam.rearrange("(c p) -> p c", p=P)[:, tiles.start : tiles.stop])
+            for c in tiles:
+                weights[c] = columns[:, c - tiles.start : c - tiles.start + 1]
+            return columns
 
         for c in range(LEAD):
             load_lines(c)
         load_w2(0)
+        weight_first = load_weights(range(0, 1), "weight_first")
         load_lines(LEAD)
         load_lines(LEAD + 1)
+        weight_others = load_weights(range(1, ROW_TILES), "weight_others")
         for part in range(1, len(W2_PARTS)):
             load_lines(LEAD + 1 + part)
             load_w2(part)
 
-        identity = kept([P, P], F32, "identity")
-        make_identity(nc, identity[:])
-        turned = psum_y.tile([P, HALF], F32, name="y_bank")
-        nc.tensor.transpose(turned[:, 0:P], vector_rows[:], identity[:])
-        vectors = kept([P, PACK + ROW_TILES], F32, "vectors")
-        nc.scalar.copy(vectors[:], turned[:, 0 : PACK + ROW_TILES])
-        bias = vectors[:, 0:PACK]
-        weight = vectors[:, PACK : PACK + ROW_TILES]
-
-        def reorder_columns(into, raw, words):
+        def reorder_columns(into, raw, pair_dtype):
             nc.scalar.copy(
-                into.bitcast(U32).rearrange("p (a t b w) -> p a t b w", a=PASSES, t=PACK, w=words),
-                raw.bitcast(U32).rearrange("p (a b t w) -> p a t b w", a=PASSES, t=PACK, w=words),
+                into.bitcast(pair_dtype).rearrange("p (a t m) -> p a m t", a=PASSES, t=PACK),
+                raw.bitcast(pair_dtype).rearrange("p (a m t) -> p a m t", a=PASSES, t=PACK),
             )
 
         w1_codes = kept([P, PASSES * 2 * H], U8, "w1_codes")
-        reorder_columns(w1_codes[:], w1_raw[:].rearrange("p a c -> p (a c)"), 2 * RUN // 4)
+        reorder_columns(w1_codes[:], w1_raw[:].rearrange("p a c -> p (a c)"), U32)
+        w1_planes = kept([P, PASSES * H], U8, "w1_planes")
+        reorder_columns(w1_planes[:], w1_scales_raw[:], U16)
 
         def list_half(half):
             return offsets[:, half * LIST_COLS : (half + 1) * LIST_COLS]
@@ -152,8 +155,6 @@ def tile_list_cine_line_refill_kernel(
 
         v_codes0 = kept([P, S], U32, "v_codes0")
         nc.vector.tensor_copy(v_codes0[:], word_windows[0][:].indirect(offsets[:]))
-        w1_planes = kept([P, PASSES * H], U8, "w1_planes")
-        reorder_columns(w1_planes[:], w1_scales_raw[:], RUN // 4)
         v_codes1 = [kept([P, HALF], U32, f"v_codes1_{half}") for half in range(HALVES)]
         for half in range(HALVES):
             nc.vector.tensor_copy(v_codes1[half][:], word_windows[1][:].indirect(list_half(half)))
@@ -190,7 +191,7 @@ def tile_list_cine_line_refill_kernel(
                         stop=(a == passes[-1]),
                     )
             for t in range(PACK):
-                nc.scalar.activation(rounded[:, t, :], sums[t][:], IDENTITY, bias=bias[:, t : t + 1])
+                nc.scalar.activation(rounded[:, t, :], sums[t][:], IDENTITY, bias=bias[:, PAIR * t : PAIR * t + 1])
             grouped = kept([P, HALF * PACK], BF16, f"h_grouped{half}")
             interleave(grouped, rounded[:])
             return grouped
@@ -225,16 +226,16 @@ def tile_list_cine_line_refill_kernel(
                 start=True,
                 stop=True,
             )
-            nc.scalar.activation(into, y_sum[:], COPY, scale=weight[:, c : c + 1])
+            nc.scalar.activation(into, y_sum[:], COPY, scale=weights[c])
 
         def store(c):
             nc.sync.dma_start(out[c * P : (c + 1) * P, :], lines[c][:])
 
         rest = {}
 
-        def complement(tiles, name, at):
+        def complement(tiles, weight, name, at):
             columns = placed([P, len(tiles)], F32, name, at)
-            nc.scalar.activation(columns[:], weight[:, tiles.start : tiles.stop], COPY, scale=-1.0, bias=1.0)
+            nc.scalar.activation(columns[:], weight[:], COPY, scale=-1.0, bias=1.0)
             for c in tiles:
                 rest[c] = columns[:, c - tiles.start : c - tiles.start + 1]
 
@@ -261,7 +262,7 @@ def tile_list_cine_line_refill_kernel(
         quantise_w2(0, after="h_rounded0")
         h = [quantise_h(0, grouped, behind_w2(0, [P, HALF], U8, "h_plane0", 2 * ALIGN))]
         gather_lines(LEAD, behind_w2(0, [P, S], F32, "held_first", ALIGN - HELD_BYTES))
-        complement(range(0, 1), "rest_first", W2_FIRST_AT + ALIGN)
+        complement(range(0, 1), weight_first, "rest_first", W2_FIRST_AT + ALIGN)
         refill_half(0)
         gather_lines(LEAD + 1, own_held(LEAD + 1))
 
@@ -269,7 +270,7 @@ def tile_list_cine_line_refill_kernel(
         h.append(quantise_h(1, grouped, behind_w2(1, [P, HALF], U8, "h_plane1", 2 * ALIGN)))
         quantise_w2(1)
         gather_lines(LEAD + 2, behind_w2(1, [P, S], F32, "held_second", ALIGN - HELD_BYTES))
-        complement(range(1, ROW_TILES), "rest_others", W2_SECOND_AT + ALIGN)
+        complement(range(1, ROW_TILES), weight_others, "rest_others", W2_SECOND_AT + ALIGN)
         refill_half(1)
         store(0)
         refill(1)

@@ -28,7 +28,7 @@ LIST_COLS = HALF // 16
 ROW_TILES = N // P
 ALIGN = 64
 PARKED = 16
-LEAD = 3
+LEAD = 4
 W2_PARTS = (128, 128, 256, 512)
 AHEAD_BANKS = 2
 MOVED_BUFS = 4
@@ -133,7 +133,8 @@ def tile_list_cine_line_refill_kernel(
         load_lines(LEAD + 1)
         weight_others = load_weights(range(1, ROW_TILES), "weight_others")
         for part in range(1, len(W2_PARTS)):
-            load_lines(LEAD + 1 + part)
+            if LEAD + 1 + part < ROW_TILES:
+                load_lines(LEAD + 1 + part)
             load_w2(part)
 
         def reorder_columns(into, raw, pair_dtype):
@@ -278,7 +279,8 @@ def tile_list_cine_line_refill_kernel(
         for part in range(HALVES, len(W2_PARTS)):
             quantise_w2(part)
             c = LEAD + 1 + part
-            gather_lines(c, own_held(c, f"w2_raw{part}"))
+            if c < ROW_TILES:
+                gather_lines(c, own_held(c, f"w2_raw{part}"))
 
         for c in range(HALVES, ROW_TILES):
             refill(c)

@@ -29,7 +29,7 @@ ROW_TILES = N // P
 ALIGN = 64
 PARKED = 16
 LEAD = 4
-W2_PARTS = (128, 128, 256, 512)
+W2_PARTS = (128, 384, 512)
 AHEAD_BANKS = 2
 MOVED_BUFS = 4
 BANKS = 4
@@ -133,9 +133,8 @@ def tile_list_cine_line_refill_kernel(
         load_lines(LEAD + 1)
         weight_others = load_weights(range(1, ROW_TILES), "weight_others")
         for part in range(1, len(W2_PARTS)):
-            if LEAD + 1 + part < ROW_TILES:
-                load_lines(LEAD + 1 + part)
             load_w2(part)
+            load_lines(LEAD + 1 + part)
 
         def reorder_columns(into, raw, pair_dtype):
             nc.scalar.copy(
@@ -154,11 +153,9 @@ def tile_list_cine_line_refill_kernel(
         def entries(half):
             return slice(half * HALF, (half + 1) * HALF)
 
-        v_codes0 = kept([P, S], U32, "v_codes0")
-        nc.vector.tensor_copy(v_codes0[:], word_windows[0][:].indirect(offsets[:]))
-        v_codes1 = [kept([P, HALF], U32, f"v_codes1_{half}") for half in range(HALVES)]
-        for half in range(HALVES):
-            nc.vector.tensor_copy(v_codes1[half][:], word_windows[1][:].indirect(list_half(half)))
+        v_codes = [kept([P, S], U32, f"v_codes{a}") for a in range(PASSES)]
+        for a in range(PASSES):
+            nc.vector.tensor_copy(v_codes[a][:], word_windows[a][:].indirect(offsets[:]))
 
         def interleave(grouped, slots):
             nc.scalar.copy(
@@ -177,7 +174,6 @@ def tile_list_cine_line_refill_kernel(
 
         def make_h(half, rounded):
             sums = [psum_h.tile([P, HALF], F32, name="h_bank") for t in range(PACK)]
-            moving = [v_codes0[:, entries(half)], v_codes1[half][:]]
             for t in range(PACK):
                 passes = (0, 1) if t < AHEAD_BANKS else (1, 0)
                 for a in passes:
@@ -186,7 +182,7 @@ def tile_list_cine_line_refill_kernel(
                         out=sums[t][:],
                         lhsT=w1_codes[:, 2 * first : 2 * (first + P)].bitcast(E2M1),
                         lhsT_scale=w1_planes[:, first : first + P],
-                        rhs=moving[a].bitcast(E4M3),
+                        rhs=v_codes[a][:, entries(half)].bitcast(E4M3),
                         rhs_scale=v_planes[a][:, entries(half)],
                         start=(a == passes[0]),
                         stop=(a == passes[-1]),
@@ -276,11 +272,8 @@ def tile_list_cine_line_refill_kernel(
         store(0)
         refill(1)
 
-        for part in range(HALVES, len(W2_PARTS)):
-            quantise_w2(part)
-            c = LEAD + 1 + part
-            if c < ROW_TILES:
-                gather_lines(c, own_held(c, f"w2_raw{part}"))
+        quantise_w2(2)
+        gather_lines(LEAD + 3, own_held(LEAD + 3, "w2_raw2"))
 
         for c in range(HALVES, ROW_TILES):
             refill(c)

@@ -18,26 +18,26 @@ IDENTITY = mybir.ActivationFunctionType.Identity
 ADD = mybir.AluOpType.add
 
 P = 128
+QUADRANT = 32
 PACK = 4
 PAIR = 2
 SPAN = PACK * PAIR
 PASSES = K // (P * PACK)
+ROW_STEP = 4
+AHEAD_BANKS = 2
 HALF = 512
 HALVES = S // HALF
 LIST_COLS = HALF // 16
 ROW_TILES = N // P
 ALIGN = 64
-PARKED = 16
 LEAD = 4
 W2_PARTS = (128, 384, 512)
-AHEAD_BANKS = 2
 MOVED_BUFS = 4
-BANKS = 4
+BANKS = 8
 
 HELD_BYTES = 4 * S
 W2_FIRST_AT = HELD_BYTES - ALIGN
-H_ROUNDED1_AT = W2_FIRST_AT + 4 * PACK * W2_PARTS[0] - ALIGN
-W2_SECOND_AT = H_ROUNDED1_AT + 2 * PACK * HALF + HELD_BYTES - ALIGN
+W2_SECOND_AT = W2_FIRST_AT + 4 * PACK * W2_PARTS[0] + HELD_BYTES - ALIGN
 W2_AT = (W2_FIRST_AT, W2_SECOND_AT)
 
 
@@ -49,8 +49,7 @@ def tile_list_cine_line_refill_kernel(
         keep = ctx.enter_context(tc.tile_pool(name="keep", bufs=1))
         staged = ctx.enter_context(tc.tile_pool(name="staged", bufs=1))
         ring = ctx.enter_context(tc.tile_pool(name="ring", bufs=MOVED_BUFS))
-        psum_h = ctx.enter_context(tc.psum_pool(name="psum_h", bufs=BANKS))
-        psum_y = ctx.enter_context(tc.psum_pool(name="psum_y", bufs=BANKS))
+        psum = ctx.enter_context(tc.psum_pool(name="psum", bufs=BANKS))
 
         def placed(shape, dtype, name, at):
             return staged.tile(shape, dtype, name=name, offset=at, align_bytes=ALIGN)
@@ -60,47 +59,59 @@ def tile_list_cine_line_refill_kernel(
 
         offsets = keep.tile([P, S // 16], U16, name="offsets")
         scale_window = kept([P, T], U8, "scale_window")
-        w1_scales_raw = kept([P, PASSES * H], U8, "w1_scales_raw")
         nc.vector.memset(scale_window[:].bitcast(I32), 0)
-        nc.vector.memset(w1_scales_raw[:].bitcast(I32), 0)
-
         w1_raw = kept([P, PASSES, 2 * H], U8, "w1_raw")
         nc.sync.dma_start(w1_raw[:].bitcast(I32), w1_words.rearrange("a p c -> p a c").bitcast(I32))
         nc.sync.dma_start(offsets[:], offs)
-        tab_rows = tab_scales.rearrange("a (q r) t -> r q a t", r=PACK)
-        for r in range(PACK):
-            nc.sync.dma_start(scale_window[r:P:PARKED, :].bitcast(I32), tab_rows[r].bitcast(I32))
-        word_windows = [kept([P, T], U32, f"word_window{a}") for a in range(PASSES)]
-        lines = {}
 
-        def load_words(a):
-            nc.sync.dma_start(word_windows[a][:].bitcast(I32), tab_words[a].rearrange("p t i -> p (t i)").bitcast(I32))
+        nc.sync.dma_start(scale_window[0:P:ROW_STEP, :].bitcast(I32), tab_scales.rearrange("a b t -> b a t").bitcast(I32))
+        v_scales = kept([P, S], U8, "v_scales")
+        w1_scales_raw = kept([P, PASSES * H], U8, "w1_scales_raw")
+        nc.vector.memset(w1_scales_raw[:].bitcast(I32), 0)
+        nc.vector.tensor_copy(v_scales[:], scale_window[:].indirect(offsets[:]))
+
+        v_codes = {}
+
+        def fetch_words(a):
+            window = kept([P, T], U32, f"word_window{a}")
+            nc.sync.dma_start(window[:].bitcast(I32), tab_words[a].rearrange("p t i -> p (t i)").bitcast(I32))
+            v_codes[a] = kept([P, S], U32, f"v_codes{a}")
+            nc.vector.tensor_copy(v_codes[a][:], window[:].indirect(offsets[:]))
+
+        lines = {}
 
         def load_lines(c):
             lines[c] = kept([P, T], F32, f"lines{c}")
             nc.sync.dma_start(lines[c][:], gT[c * P : (c + 1) * P, :])
 
-        load_words(0)
-        w1_rows = w1_scales.rearrange("a (q r) c -> r q a c", r=PACK)
-        for r in range(PACK):
-            nc.sync.dma_start(
-                w1_scales_raw[r:P:32, :].rearrange("q (a c) -> q a c", a=PASSES).bitcast(I32),
-                w1_rows[r].bitcast(I32),
-            )
-        load_words(1)
+        def entries(half):
+            return slice(half * HALF, (half + 1) * HALF)
 
         bias = kept([P, SPAN], F32, "bias")
-        for e in range(PAIR):
-            nc.sync.dma_start(
-                bias[e:P:PAIR, 0 : SPAN - 1], b1.rearrange("(m x) -> m x", x=SPAN)[:, e : e + SPAN - 1]
-            )
 
-        v_plane0 = kept([P, S], U8, "v_plane0")
-        v_plane1 = kept([P, S], U8, "v_plane1")
-        nc.vector.tensor_copy(v_plane0[:], scale_window[:].indirect(offsets[:]))
-        for r in range(PACK):
-            nc.sync.dma_start(v_plane1[r:P:32, :].bitcast(I32), v_plane0[PARKED + r : P : 32, :].bitcast(I32))
-        v_planes = [v_plane0, v_plane1]
+        def load_bias():
+            for e in range(PAIR):
+                nc.scalar.dma_start(
+                    bias[e:P:PAIR, 0 : SPAN - 1], b1.rearrange("(m x) -> m x", x=SPAN)[:, e : e + SPAN - 1]
+                )
+
+        def load_w1_scales():
+            w1_rows = w1_scales.rearrange("a (q r) c -> r q a c", r=PACK)
+            for r in range(PACK):
+                nc.scalar.dma_start(
+                    w1_scales_raw[r:P:QUADRANT, :].rearrange("q (a c) -> q a c", a=PASSES).bitcast(I32),
+                    w1_rows[r].bitcast(I32),
+                )
+
+        v_planes = {}
+
+        def lay_planes(half, queue):
+            v_planes[half] = kept([P, PASSES * HALF], U8, f"v_planes{half}")
+            for q in (0, 2, 1, 3):
+                queue.dma_start(
+                    v_planes[half][q * QUADRANT : q * QUADRANT + PACK, :].bitcast(I32),
+                    v_scales[q * QUADRANT : (q + 1) * QUADRANT : ROW_STEP, entries(half)].bitcast(I32),
+                )
 
         w2_rows = w2.rearrange("(m t e) n -> e m t n", t=PACK, e=PAIR)
         w2_raw = [placed([P, PACK, W2_PARTS[part]], F32, f"w2_raw{part}", W2_AT[part]) for part in range(HALVES)]
@@ -117,24 +128,31 @@ def tile_list_cine_line_refill_kernel(
 
         weights = {}
 
-        def load_weights(tiles, name):
+        def load_weights(tiles, name, queue):
             columns = kept([P, len(tiles)], F32, name)
             with nc.allow_non_contiguous_dma(reason="one value for each partition"):
-                nc.sync.dma_start(columns[:], lam.rearrange("(c p) -> p c", p=P)[:, tiles.start : tiles.stop])
+                queue.dma_start(columns[:], lam.rearrange("(c p) -> p c", p=P)[:, tiles.start : tiles.stop])
             for c in tiles:
                 weights[c] = columns[:, c - tiles.start : c - tiles.start + 1]
             return columns
 
+        fetch_words(0)
+        load_w1_scales()
+        fetch_words(1)
+        load_bias()
+        lay_planes(0, nc.scalar)
         for c in range(LEAD):
             load_lines(c)
+        weight_first = load_weights(range(0, 1), "weight_first", nc.scalar)
         load_w2(0)
-        weight_first = load_weights(range(0, 1), "weight_first")
         load_lines(LEAD)
-        load_lines(LEAD + 1)
-        weight_others = load_weights(range(1, ROW_TILES), "weight_others")
-        for part in range(1, len(W2_PARTS)):
-            load_w2(part)
-            load_lines(LEAD + 1 + part)
+        lay_planes(1, nc.sync)
+        for c in range(LEAD + 1, ROW_TILES - 1):
+            load_lines(c)
+        load_w2(1)
+        load_lines(ROW_TILES - 1)
+        weight_others = load_weights(range(1, ROW_TILES), "weight_others", nc.sync)
+        load_w2(2)
 
         def reorder_columns(into, raw, pair_dtype):
             nc.scalar.copy(
@@ -150,16 +168,9 @@ def tile_list_cine_line_refill_kernel(
         def list_half(half):
             return offsets[:, half * LIST_COLS : (half + 1) * LIST_COLS]
 
-        def entries(half):
-            return slice(half * HALF, (half + 1) * HALF)
-
-        v_codes = [kept([P, S], U32, f"v_codes{a}") for a in range(PASSES)]
-        for a in range(PASSES):
-            nc.vector.tensor_copy(v_codes[a][:], word_windows[a][:].indirect(offsets[:]))
-
         def interleave(grouped, slots):
             nc.scalar.copy(
-                grouped[:].rearrange("p (u i t) -> p u t i", t=PACK, i=4),
+                grouped.rearrange("p (u i t) -> p u t i", t=PACK, i=4),
                 slots.rearrange("p t (u i) -> p u t i", i=4),
             )
 
@@ -168,12 +179,13 @@ def tile_list_cine_line_refill_kernel(
 
         def quantise_w2(part, after=None):
             grouped = kept([P, W2_PARTS[part] * PACK], BF16, f"w2_grouped{part}", after)
-            interleave(grouped, w2_raw[part][:])
+            interleave(grouped[:], w2_raw[part][:])
             columns = w2_columns(part)
             nc.vector.quantize_mx(out=w2_codes[:, columns].bitcast(E4M3), scales=w2_plane[:, columns], in_=grouped[:])
 
-        def make_h(half, rounded):
-            sums = [psum_h.tile([P, HALF], F32, name="h_bank") for t in range(PACK)]
+        def make_h(half):
+            rounded = kept([P, PACK, HALF], BF16, f"h_rounded{half}")
+            sums = [psum.tile([P, HALF], F32, name="bank") for t in range(PACK)]
             for t in range(PACK):
                 passes = (0, 1) if t < AHEAD_BANKS else (1, 0)
                 for a in passes:
@@ -183,14 +195,18 @@ def tile_list_cine_line_refill_kernel(
                         lhsT=w1_codes[:, 2 * first : 2 * (first + P)].bitcast(E2M1),
                         lhsT_scale=w1_planes[:, first : first + P],
                         rhs=v_codes[a][:, entries(half)].bitcast(E4M3),
-                        rhs_scale=v_planes[a][:, entries(half)],
+                        rhs_scale=v_planes[half][:, a * HALF : (a + 1) * HALF],
                         start=(a == passes[0]),
                         stop=(a == passes[-1]),
                     )
             for t in range(PACK):
                 nc.scalar.activation(rounded[:, t, :], sums[t][:], IDENTITY, bias=bias[:, PAIR * t : PAIR * t + 1])
-            grouped = kept([P, HALF * PACK], BF16, f"h_grouped{half}")
-            interleave(grouped, rounded[:])
+            return rounded
+
+        def group_h(rounded, grouped, pieces):
+            width = HALF // pieces
+            for first in range(0, HALF, width):
+                interleave(grouped[:, PACK * first : PACK * (first + width)], rounded[:, :, first : first + width])
             return grouped
 
         def quantise_h(half, grouped, plane):
@@ -213,7 +229,7 @@ def tile_list_cine_line_refill_kernel(
         def predict(c, half, into):
             codes, plane = h[half]
             rows = slice(c * P, (c + 1) * P)
-            y_sum = psum_y.tile([P, HALF], F32, name="y_bank")
+            y_sum = psum.tile([P, HALF], F32, name="bank")
             nc.tensor.matmul_mx(
                 out=y_sum[:],
                 lhsT=w2_codes[:, rows].bitcast(E4M3),
@@ -255,25 +271,24 @@ def tile_list_cine_line_refill_kernel(
 
         for c in range(LEAD):
             gather_lines(c, own_held(c))
-        grouped = make_h(0, kept([P, PACK, HALF], BF16, "h_rounded0"))
+        grouped = group_h(make_h(0), kept([P, HALF * PACK], BF16, "h_grouped0"), 1)
         quantise_w2(0, after="h_rounded0")
         h = [quantise_h(0, grouped, behind_w2(0, [P, HALF], U8, "h_plane0", 2 * ALIGN))]
         gather_lines(LEAD, behind_w2(0, [P, S], F32, "held_first", ALIGN - HELD_BYTES))
         complement(range(0, 1), weight_first, "rest_first", W2_FIRST_AT + ALIGN)
         refill_half(0)
-        gather_lines(LEAD + 1, own_held(LEAD + 1))
 
-        grouped = make_h(1, placed([P, PACK, HALF], BF16, "h_rounded1", H_ROUNDED1_AT))
+        for c in range(LEAD + 1, ROW_TILES - 1):
+            gather_lines(c, own_held(c))
+        grouped = group_h(make_h(1), kept([P, HALF * PACK], BF16, "h_grouped1"), 1)
         h.append(quantise_h(1, grouped, behind_w2(1, [P, HALF], U8, "h_plane1", 2 * ALIGN)))
         quantise_w2(1)
-        gather_lines(LEAD + 2, behind_w2(1, [P, S], F32, "held_second", ALIGN - HELD_BYTES))
+        gather_lines(ROW_TILES - 1, behind_w2(1, [P, S], F32, "held_second", ALIGN - HELD_BYTES))
         complement(range(1, ROW_TILES), weight_others, "rest_others", W2_SECOND_AT + ALIGN)
         refill_half(1)
         store(0)
         refill(1)
 
         quantise_w2(2)
-        gather_lines(LEAD + 3, own_held(LEAD + 3, "w2_raw2"))
-
         for c in range(HALVES, ROW_TILES):
             refill(c)

from contextlib import ExitStack

import concourse.mybir as mybir

K, T, S, H, N = 1024, 2048, 1024, 512, 1024
FLOPS = 2 * K * H * S + 2 * H * N * S

F32 = mybir.dt.float32
BF16 = mybir.dt.bfloat16
I32 = mybir.dt.int32
U32 = mybir.dt.uint32
U16 = mybir.dt.uint16
U8 = mybir.dt.uint8
E4M3 = mybir.dt.float8_e4m3fn_x4
E2M1 = mybir.dt.float4_e2m1fn_x4
COPY = mybir.ActivationFunctionType.Copy
IDENTITY = mybir.ActivationFunctionType.Identity
ADD = mybir.AluOpType.add

P = 128
QUADRANT = 32
PACK = 4
PAIR = 2
SPAN = PACK * PAIR
PASSES = K // (P * PACK)
ROW_STEP = 4
AHEAD_BANKS = 2
HALF = 512
HALVES = S // HALF
LIST_COLS = HALF // 16
ROW_TILES = N // P
ALIGN = 64
LEAD = 4
W2_PARTS = (128, 384, 512)
MOVED_BUFS = 4
BANKS = 8

HELD_BYTES = 4 * S
W2_FIRST_AT = HELD_BYTES - ALIGN
W2_SECOND_AT = W2_FIRST_AT + 4 * PACK * W2_PARTS[0] + HELD_BYTES - ALIGN
W2_AT = (W2_FIRST_AT, W2_SECOND_AT)


def tile_list_cine_line_refill_kernel(
    tc, tab_words, tab_scales, w1_words, w1_scales, b1, w2, lam, gT, offs, out
):
    nc = tc.nc
    with ExitStack() as ctx:
        keep = ctx.enter_context(tc.tile_pool(name="keep", bufs=1))
        staged = ctx.enter_context(tc.tile_pool(name="staged", bufs=1))
        ring = ctx.enter_context(tc.tile_pool(name="ring", bufs=MOVED_BUFS))
        psum = ctx.enter_context(tc.psum_pool(name="psum", bufs=BANKS))

        def placed(shape, dtype, name, at):
            return staged.tile(shape, dtype, name=name, offset=at, align_bytes=ALIGN)

        def kept(shape, dtype, name, after=None):
            return keep.tile(shape, dtype, name=name, tag=after or name, align_bytes=ALIGN)

        offsets = keep.tile([P, S // 16], U16, name="offsets")
        scale_window = kept([P, T], U8, "scale_window")
        nc.vector.memset(scale_window[:].bitcast(I32), 0)
        w1_raw = kept([P, PASSES, 2 * H], U8, "w1_raw")
        nc.sync.dma_start(w1_raw[:].bitcast(I32), w1_words.rearrange("a p c -> p a c").bitcast(I32))
        nc.sync.dma_start(offsets[:], offs)

        nc.sync.dma_start(scale_window[0:P:ROW_STEP, :].bitcast(I32), tab_scales.rearrange("a b t -> b a t").bitcast(I32))
        v_scales = kept([P, S], U8, "v_scales")
        w1_scales_raw = kept([P, PASSES * H], U8, "w1_scales_raw")
        nc.vector.memset(w1_scales_raw[:].bitcast(I32), 0)
        nc.vector.tensor_copy(v_scales[:], scale_window[:].indirect(offsets[:]))

        v_codes = {}

        def fetch_words(a):
            window = kept([P, T], U32, f"word_window{a}")
            nc.sync.dma_start(window[:].bitcast(I32), tab_words[a].rearrange("p t i -> p (t i)").bitcast(I32))
            v_codes[a] = kept([P, S], U32, f"v_codes{a}")
            nc.vector.tensor_copy(v_codes[a][:], window[:].indirect(offsets[:]))

        lines = {}

        def load_lines(c):
            lines[c] = kept([P, T], F32, f"lines{c}")
            nc.sync.dma_start(lines[c][:], gT[c * P : (c + 1) * P, :])

        def entries(half):
            return slice(half * HALF, (half + 1) * HALF)

        bias = kept([P, SPAN], F32, "bias")

        def load_bias():
            for e in range(PAIR):
                nc.scalar.dma_start(
                    bias[e:P:PAIR, 0 : SPAN - 1], b1.rearrange("(m x) -> m x", x=SPAN)[:, e : e + SPAN - 1]
                )

        def load_w1_scales():
            w1_rows = w1_scales.rearrange("a (q r) c -> r q a c", r=PACK)
            for r in range(PACK):
                nc.scalar.dma_start(
                    w1_scales_raw[r:P:QUADRANT, :].rearrange("q (a c) -> q a c", a=PASSES).bitcast(I32),
                    w1_rows[r].bitcast(I32),
                )

        v_planes = {}

        def lay_planes(half, queue):
            v_planes[half] = kept([P, PASSES * HALF], U8, f"v_planes{half}")
            for q in (0, 2, 1, 3):
                queue.dma_start(
                    v_planes[half][q * QUADRANT : q * QUADRANT + PACK, :].bitcast(I32),
                    v_scales[q * QUADRANT : (q + 1) * QUADRANT : ROW_STEP, entries(half)].bitcast(I32),
                )

        w2_rows = w2.rearrange("(m t e) n -> e m t n", t=PACK, e=PAIR)
        w2_raw = [placed([P, PACK, W2_PARTS[part]], F32, f"w2_raw{part}", W2_AT[part]) for part in range(HALVES)]
        for part in range(HALVES, len(W2_PARTS)):
            w2_raw.append(kept([P, PACK, W2_PARTS[part]], F32, f"w2_raw{part}"))

        def w2_columns(part):
            first = sum(W2_PARTS[:part])
            return slice(first, first + W2_PARTS[part])

        def load_w2(part):
            for e in range(PAIR):
                nc.sync.dma_start(w2_raw[part][e:P:PAIR, :, :], w2_rows[e, :, :, w2_columns(part)])

        weights = {}

        def load_weights(tiles, name, queue):
            columns = kept([P, len(tiles)], F32, name)
            with nc.allow_non_contiguous_dma(reason="one value for each partition"):
                queue.dma_start(columns[:], lam.rearrange("(c p) -> p c", p=P)[:, tiles.start : tiles.stop])
            for c in tiles:
                weights[c] = columns[:, c - tiles.start : c - tiles.start + 1]
            return columns

        fetch_words(0)
        load_w1_scales()
        fetch_words(1)
        load_bias()
        lay_planes(0, nc.scalar)
        for c in range(LEAD):
            load_lines(c)
        weight_first = load_weights(range(0, 1), "weight_first", nc.scalar)
        load_w2(0)
        load_lines(LEAD)
        lay_planes(1, nc.sync)
        for c in range(LEAD + 1, ROW_TILES - 1):
            load_lines(c)
        load_w2(1)
        load_lines(ROW_TILES - 1)
        weight_others = load_weights(range(1, ROW_TILES), "weight_others", nc.sync)
        load_w2(2)

        def reorder_columns(into, raw, pair_dtype):
            nc.scalar.copy(
                into.bitcast(pair_dtype).rearrange("p (a t m) -> p a m t", a=PASSES, t=PACK),
                raw.bitcast(pair_dtype).rearrange("p (a m t) -> p a m t", a=PASSES, t=PACK),
            )

        w1_codes = kept([P, PASSES * 2 * H], U8, "w1_codes")
        reorder_columns(w1_codes[:], w1_raw[:].rearrange("p a c -> p (a c)"), U32)
        w1_planes = kept([P, PASSES * H], U8, "w1_planes")
        reorder_columns(w1_planes[:], w1_scales_raw[:], U16)

        def list_half(half):
            return offsets[:, half * LIST_COLS : (half + 1) * LIST_COLS]

        def interleave(grouped, slots):
            nc.scalar.copy(
                grouped.rearrange("p (u i t) -> p u t i", t=PACK, i=4),
                slots.rearrange("p t (u i) -> p u t i", i=4),
            )

        w2_codes = kept([P, N], U32, "w2_codes")
        w2_plane = kept([P, N], U8, "w2_plane")

        def quantise_w2(part, after=None):
            grouped = kept([P, W2_PARTS[part] * PACK], BF16, f"w2_grouped{part}", after)
            interleave(grouped[:], w2_raw[part][:])
            columns = w2_columns(part)
            nc.vector.quantize_mx(out=w2_codes[:, columns].bitcast(E4M3), scales=w2_plane[:, columns], in_=grouped[:])

        def make_h(half):
            rounded = kept([P, PACK, HALF], BF16, f"h_rounded{half}")
            sums = [psum.tile([P, HALF], F32, name="bank") for t in range(PACK)]
            for t in range(PACK):
                passes = (0, 1) if t < AHEAD_BANKS else (1, 0)
                for a in passes:
                    first = a * H + t * P
                    nc.tensor.matmul_mx(
                        out=sums[t][:],
                        lhsT=w1_codes[:, 2 * first : 2 * (first + P)].bitcast(E2M1),
                        lhsT_scale=w1_planes[:, first : first + P],
                        rhs=v_codes[a][:, entries(half)].bitcast(E4M3),
                        rhs_scale=v_planes[half][:, a * HALF : (a + 1) * HALF],
                        start=(a == passes[0]),
                        stop=(a == passes[-1]),
                    )
            for t in range(PACK):
                nc.scalar.activation(rounded[:, t, :], sums[t][:], IDENTITY, bias=bias[:, PAIR * t : PAIR * t + 1])
            return rounded

        def group_h(rounded, grouped, pieces):
            width = HALF // pieces
            for first in range(0, HALF, width):
                interleave(grouped[:, PACK * first : PACK * (first + width)], rounded[:, :, first : first + width])
            return grouped

        def quantise_h(half, grouped, plane):
            codes = kept([P, HALF], U32, f"h_codes{half}")
            nc.vector.quantize_mx(out=codes[:].bitcast(E4M3), scales=plane[:], in_=grouped[:])
            return codes, plane

        held = {}

        def gather_lines(c, into):
            held[c] = into
            nc.vector.tensor_copy(into[:], lines[c][:].indirect(offsets[:]))

        def own_held(c, after=None):
            return kept([P, S], F32, f"held{c}", after)

        def weigh_held(c, columns):
            nc.scalar.activation(held[c][:, columns], held[c][:, columns], COPY, scale=rest[c])

        def predict(c, half, into):
            codes, plane = h[half]
            rows = slice(c * P, (c + 1) * P)
            y_sum = psum.tile([P, HALF], F32, name="bank")
            nc.tensor.matmul_mx(
                out=y_sum[:],
                lhsT=w2_codes[:, rows].bitcast(E4M3),
                lhsT_scale=w2_plane[:, rows],
                rhs=codes[:].bitcast(E4M3),
                rhs_scale=plane[:],
                start=True,
                stop=True,
            )
            nc.scalar.activation(into, y_sum[:], COPY, scale=weights[c])

        def store(c):
            nc.sync.dma_start(out[c * P : (c + 1) * P, :], lines[c][:])

        rest = {}

        def complement(tiles, weight, name, at):
            columns = placed([P, len(tiles)], F32, name, at)
            nc.scalar.activation(columns[:], weight[:], COPY, scale=-1.0, bias=1.0)
            for c in tiles:
                rest[c] = columns[:, c - tiles.start : c - tiles.start + 1]

        def refill_half(half):
            moved = kept([P, HALF], F32, f"moved_half{half}")
            weigh_held(0, entries(half))
            predict(0, half, moved[:])
            nc.vector.tensor_tensor(lines[0][:].indirect(list_half(half)), held[0][:, entries(half)], moved[:], ADD)

        def refill(c):
            weigh_held(c, slice(0, S))
            moved = ring.tile([P, S], F32, name="moved")
            for half in range(HALVES):
                predict(c, half, moved[:, entries(half)])
            nc.vector.tensor_tensor(lines[c][:].indirect(offsets[:]), held[c][:], moved[:], ADD)
            store(c)

        def behind_w2(part, shape, dtype, name, past):
            return placed(shape, dtype, name, W2_AT[part] + past)

        for c in range(LEAD):
            gather_lines(c, own_held(c))
        grouped = group_h(make_h(0), kept([P, HALF * PACK], BF16, "h_grouped0"), 1)
        quantise_w2(0, after="h_rounded0")
        h = [quantise_h(0, grouped, behind_w2(0, [P, HALF], U8, "h_plane0", 2 * ALIGN))]
        gather_lines(LEAD, behind_w2(0, [P, S], F32, "held_first", ALIGN - HELD_BYTES))
        complement(range(0, 1), weight_first, "rest_first", W2_FIRST_AT + ALIGN)
        refill_half(0)

        for c in range(LEAD + 1, ROW_TILES - 1):
            gather_lines(c, own_held(c))
        grouped = group_h(make_h(1), kept([P, HALF * PACK], BF16, "h_grouped1"), 1)
        h.append(quantise_h(1, grouped, behind_w2(1, [P, HALF], U8, "h_plane1", 2 * ALIGN)))
        quantise_w2(1)
        gather_lines(ROW_TILES - 1, behind_w2(1, [P, S], F32, "held_second", ALIGN - HELD_BYTES))
        complement(range(1, ROW_TILES), weight_others, "rest_others", W2_SECOND_AT + ALIGN)
        refill_half(1)
        store(0)
        refill(1)

        quantise_w2(2)
        for c in range(HALVES, ROW_TILES):
            refill(c)
